import numpy as np
import ml_dtypes


def mxq(x, axis, fmt="e4m3"):
    dtype, down = {"e4m3": (ml_dtypes.float8_e4m3fn, 7), "e5m2": (ml_dtypes.float8_e5m2, 14)}[fmt]
    v = np.moveaxis(np.asarray(x, np.float32).astype(ml_dtypes.bfloat16).astype(np.float64), axis, -1)
    blocks = v.reshape(v.shape[:-1] + (-1, 32))
    amax = np.abs(blocks).max(-1, keepdims=True)
    byte = np.maximum(np.where(amax > 0, np.frexp(amax)[1] - 1 + 127, 0) - down, 1)
    scale = np.exp2(byte - 127.0)
    codes = (blocks / scale).astype(np.float32).astype(dtype).astype(np.float64)
    return np.moveaxis((codes * scale).reshape(v.shape), -1, axis)


WIDE = False


def mx_kscale(k):
    if not WIDE:
        return np.ones(k)
    levels = np.array([10, -10, 5, -5, 0])
    if k % 512:
        return np.exp2(np.random.permutation(np.resize(levels, k // 32))).repeat(32)
    a = np.empty((k // 512, 16))
    for p in range(k // 512):
        a[p, :8] = np.random.permutation(np.resize(levels, 8))
        for g in range(8):
            far = levels[np.abs(levels - a[p, g]) >= 10]
            a[p, g + 8] = far[np.random.randint(len(far))]
    return np.exp2(a.ravel()).repeat(32)


def f64(x):
    return np.asarray(x).astype(np.float64)


def striped(idx):
    return np.tile(idx.reshape(-1, 16).T, (8, 1)).astype(np.uint16)


def unstriped(offs):
    return offs[:16].T.reshape(-1).astype(np.int64)


def striped8(idx):
    return np.concatenate([x.reshape(-1, 16).T for x in idx]).astype(np.uint16)


def runs(offs, k):
    lists = np.stack([offs[16 * r : 16 * r + 16].T.reshape(-1) for r in range(8)]).astype(np.int64)
    return lists[np.arange(k) % 512 // 64]


def pack_weight(w):
    k, n = w.shape
    w = f64(np.asarray(w, np.float32).astype(ml_dtypes.bfloat16)).reshape(k // 32, 32, n)
    amax = np.abs(w).max(1)
    byte = np.clip(np.where(amax > 0, np.frexp(amax)[1] - 1 + 127 - 7, 1), 1, 254)
    scaled = (w * np.exp2(127.0 - byte)[:, None, :]).reshape(k, n).astype(np.float32)
    words = np.ascontiguousarray(scaled.reshape(k // 512, 128, 4, n).transpose(0, 1, 3, 2)).astype(ml_dtypes.float8_e4m3fn).view(np.uint8)
    return words, np.ascontiguousarray(byte.astype(np.uint8).reshape(k // 512, 16, n))


def unpack_weight(words, scales):
    g, p, n, _ = words.shape
    vals = np.ascontiguousarray(words).view(ml_dtypes.float8_e4m3fn).astype(np.float64) * np.repeat(np.exp2(scales.astype(np.float64) - 127.0), 8, axis=1)[..., None]
    return vals.transpose(0, 1, 3, 2).reshape(g * 512, n)


K, T, S, V, N, H = 512, 2048, 512, 256, 512, 512


def setup_inputs():
    n = np.random.standard_normal
    s = mx_kscale(K)[:, None]
    u = mx_kscale(H)
    packed_xT = pack_weight(n((K, T)) * s)
    perm = np.stack([np.random.permutation(S) for _ in range(8)])
    return {
        "x_words": packed_xT[0],
        "x_scales": packed_xT[1],
        "w1": (n((K, H)) / np.sqrt(K) / s * u).astype(np.float32),
        "sz": np.repeat(np.random.uniform(0.2, 0.8, (8, V)), 64, axis=0).astype(np.float32),
        "w2": (n((H, N)) / np.sqrt(H) / u[:, None]).astype(np.float32),
        "offs": striped(np.random.permutation(T)[:S]),
        "la": striped8(perm[:, :V]),
        "lb": striped8(perm[:, V:]),
    }


def reference(x_words, x_scales, w1, sz, w2, offs, la, lb):
    xq = unpack_weight(x_words, x_scales)[:, unstriped(offs)]
    y = mxq(f64(w1), 0, "e4m3").T @ xq
    b = y[np.arange(H)[:, None], runs(lb, H)]
    a = y[np.arange(H)[:, None], runs(la, H)]
    mg = b + f64(sz) * (a - b)
    p = np.zeros((H, S))
    p[np.arange(H)[:, None], runs(la, H)] = mg
    zs = p.copy()
    zs[np.arange(H)[:, None], runs(lb, H)] = mg
    return mxq(f64(w2), 0, "e4m3").T @ mxq(zs, 0, "e4m3")

@@ -1,0 +1,151 @@
+from contextlib import ExitStack
+
+import concourse.mybir as mybir
+
+K, T, S, V, N, H = 512, 2048, 512, 256, 512, 512
+FLOPS = 2 * K * H * S + 2 * H * N * S
+BYTES = K * T + K * T // 32 + 4 * K * H + 4 * 8 * V + 4 * H * N + 2 * 128 * (S + 2 * V) // 16 + 4 * N * S
+
+F32 = mybir.dt.float32
+BF16 = mybir.dt.bfloat16
+I32 = mybir.dt.int32
+U32 = mybir.dt.uint32
+U16 = mybir.dt.uint16
+U8 = mybir.dt.uint8
+FP8X4 = mybir.dt.float8_e4m3fn_x4
+MULT = mybir.AluOpType.mult
+ADD = mybir.AluOpType.add
+
+P = 128
+PACK = 4
+HALF = S // 2
+
+
+def tile_picked_tomein_none_p_kernel(tc, x_words, x_scales, w1, sz, w2, offs, la, lb, out):
+    nc = tc.nc
+    with ExitStack() as ctx:
+        keep = ctx.enter_context(tc.tile_pool(name="keep", bufs=1))
+        psum = ctx.enter_context(tc.psum_pool(name="psum", bufs=1))
+
+        offs_sb = keep.tile([P, S // 16], U16, name="offs_sb")
+        la_sb = keep.tile([P, V // 16], U16, name="la_sb")
+        lb_sb = keep.tile([P, V // 16], U16, name="lb_sb")
+        word_table = keep.tile([P, T], I32, name="word_table")
+        scale_table = keep.tile([P, T], U8, name="scale_table")
+        w1_raw = [keep.tile([P, 2, H], F32, name=f"w1_raw{u}") for u in range(2)]
+        w2_raw = keep.tile([P, PACK, N], F32, name="w2_raw")
+        share_a = keep.tile([P, V], F32, name="share_a")
+        share_b = keep.tile([P, V], F32, name="share_b")
+
+        nc.vector.memset(scale_table[:].bitcast(I32), 0)
+        w1_rows = w1.rearrange("(p j) c -> p j c", j=PACK)
+        nc.sync.dma_start(offs_sb[:], offs)
+        nc.sync.dma_start(w1_raw[0][:], w1_rows[:, 0:2, :])
+        for q in range(4):
+            nc.sync.dma_start(scale_table[32 * q : 32 * q + 4, :].bitcast(I32), x_scales[0, 4 * q : 4 * q + 4, :].bitcast(I32))
+        nc.sync.dma_start(w1_raw[1][:], w1_rows[:, 2:4, :])
+        nc.sync.dma_start(word_table[:], x_words[0].rearrange("p n t -> p (n t)").bitcast(I32))
+        nc.sync.dma_start(share_a[:], sz.rearrange("(p t) v -> p t v", t=PACK)[:, 0, :])
+        nc.sync.dma_start(la_sb[:], la)
+        nc.sync.dma_start(lb_sb[:], lb)
+        nc.sync.dma_start(w2_raw[:], w2.rearrange("(p j) c -> p j c", j=PACK))
+
+        x_scale = keep.tile([P, S], U8, name="x_scale", align_bytes=64)
+        nc.vector.tensor_copy(x_scale[:], scale_table[:].indirect(offs_sb[:]))
+
+        w1_bf = keep.tile([P, H * PACK], BF16, name="w1_bf", align_bytes=64)
+        w1_dst = w1_bf[:].rearrange("p (t m j) -> p m j t", t=PACK, j=PACK)
+        nc.scalar.copy(w1_dst[:, :, 0:2, :], w1_raw[0][:].rearrange("p j (m t) -> p m j t", t=PACK))
+        nc.vector.tensor_copy(w1_dst[:, :, 2:4, :], w1_raw[1][:].rearrange("p j (m t) -> p m j t", t=PACK))
+        w1_code = keep.tile([P, H], U32, name="w1_code", align_bytes=64)
+        w1_scale = keep.tile([P, H], U8, name="w1_scale", align_bytes=64)
+        nc.vector.quantize_mx(out=w1_code[:].bitcast(FP8X4), scales=w1_scale[:], in_=w1_bf[:])
+
+        x_code = keep.tile([P, S], U32, name="x_code", align_bytes=64)
+        for h in range(2):
+            nc.vector.tensor_copy(
+                x_code[:, h * HALF : (h + 1) * HALF],
+                word_table[:].bitcast(U32).indirect(offs_sb[:, h * HALF // 16 : (h + 1) * HALF // 16]),
+            )
+        nc.vector.tensor_scalar(share_b[:], share_a[:], -1.0, 1.0, MULT, ADD)
+
+        y = [keep.tile([P, S], F32, name=f"y{t}") for t in range(PACK)]
+        order = [2, 0, 1, 3]
+        pieces = [(order[0], 0, HALF), (order[1], 0, HALF), (order[0], HALF, S), (order[1], HALF, S), (order[2], 0, S), (order[3], 0, S)]
+        for b, (t, lo, hi) in enumerate(pieces):
+            acc = psum.tile([P, hi - lo], F32, name=f"acc_y{b}", tag=f"bank{b}")
+            nc.tensor.matmul_mx(
+                out=acc[:],
+                lhsT=w1_code[:, t * P : (t + 1) * P].bitcast(FP8X4),
+                lhsT_scale=w1_scale[:, t * P : (t + 1) * P],
+                rhs=x_code[:, lo:hi].bitcast(FP8X4),
+                rhs_scale=x_scale[:, lo:hi],
+                start=True,
+                stop=True,
+            )
+            nc.scalar.copy(y[t][:, lo:hi], acc[:])
+
+        w2_bf = keep.tile([P, N * PACK], BF16, name="w2_bf", align_bytes=64)
+        w2_dst = w2_bf[:].rearrange("p (c i j) -> p c j i", i=4, j=PACK)
+        w2_src = w2_raw[:].rearrange("p j (c i) -> p c j i", i=4)
+        for u in range(2):
+            nc.scalar.copy(w2_dst[:, u * 64 : (u + 1) * 64], w2_src[:, u * 64 : (u + 1) * 64])
+        w2_code = keep.tile([P, N], U32, name="w2_code", align_bytes=64)
+        w2_scale = keep.tile([P, N], U8, name="w2_scale", align_bytes=64)
+
+        part_a = [keep.tile([P, V], F32, name=f"part_a{t}") for t in range(PACK)]
+        part_b = [keep.tile([P, V], F32, name=f"part_b{t}") for t in range(PACK)]
+        zs = {}
+        zs_bf = [keep.tile([P, HALF, PACK], BF16, name=f"zs_bf{h}", align_bytes=64) for h in range(2)]
+
+        def gather_a(t):
+            nc.vector.tensor_tensor(part_a[t][:], y[t][:].indirect(la_sb[:]), share_a[:], MULT)
+
+        def gather_b(t):
+            nc.vector.tensor_tensor(part_b[t][:], y[t][:].indirect(lb_sb[:]), share_b[:], MULT)
+
+        def scatter(t, places):
+            nc.vector.tensor_tensor(zs[t][:].indirect(places[:]), part_a[t][:], part_b[t][:], ADD)
+
+        gather_a(order[0])
+        gather_b(order[0])
+        for i, t in enumerate(order):
+            last = i + 1 == PACK
+            zs[t] = keep.tile([P, S], F32, name=f"zs{t}", tag=f"zs{min(t, 2)}")
+            if not last:
+                gather_a(order[i + 1])
+            scatter(t, la_sb)
+            if not last:
+                gather_b(order[i + 1])
+            else:
+                nc.vector.quantize_mx(out=w2_code[:].bitcast(FP8X4), scales=w2_scale[:], in_=w2_bf[:])
+            scatter(t, lb_sb)
+            if not last:
+                for h in range(2):
+                    nc.scalar.copy(zs_bf[h][:, :, t], zs[t][:, h * HALF : (h + 1) * HALF])
+
+        nc.vector.tensor_copy(zs_bf[0][:, :, PACK - 1], zs[PACK - 1][:, 0:HALF])
+        nc.scalar.copy(zs_bf[1][:, :, PACK - 1], zs[PACK - 1][:, HALF:S])
+
+        for h in range(2):
+            z_code = keep.tile([P, HALF], U32, name=f"z_code{h}", align_bytes=64)
+            z_scale = keep.tile([P, HALF], U8, name=f"z_scale{h}", align_bytes=64)
+            nc.vector.quantize_mx(out=z_code[:].bitcast(FP8X4), scales=z_scale[:], in_=zs_bf[h][:].rearrange("p c j -> p (c j)"))
+            for m in range(N // P):
+                b = h * (N // P) + m
+                acc = psum.tile([P, HALF], F32, name=f"acc_o{b}", tag=f"bank{b}")
+                nc.tensor.matmul_mx(
+                    out=acc[:],
+                    lhsT=w2_code[:, m * P : (m + 1) * P].bitcast(FP8X4),
+                    lhsT_scale=w2_scale[:, m * P : (m + 1) * P],
+                    rhs=z_code[:].bitcast(FP8X4),
+                    rhs_scale=z_scale[:],
+                    start=True,
+                    stop=True,
+                )
+                res = keep.tile([P, HALF], F32, name=f"res{b}")
+                if b % 2 == 0:
+                    nc.vector.tensor_copy(res[:], acc[:])
+                else:
+                    nc.scalar.copy(res[:], acc[:])
+                nc.sync.dma_start(out[m * P : (m + 1) * P, h * HALF : (h + 1) * HALF], res[:])

@@ -15,10 +15,12 @@ U8 = mybir.dt.uint8
 FP8X4 = mybir.dt.float8_e4m3fn_x4
 MULT = mybir.AluOpType.mult
 ADD = mybir.AluOpType.add
+COPY = mybir.ActivationFunctionType.Copy
 
 P = 128
 PACK = 4
 HALF = S // 2
+QUART = S // 4
 
 
 def tile_picked_tomein_none_p_kernel(tc, x_words, x_scales, w1, sz, w2, offs, la, lb, out):
@@ -26,6 +28,17 @@ def tile_picked_tomein_none_p_kernel(tc, x_words, x_scales, w1, sz, w2, offs, la
     with ExitStack() as ctx:
         keep = ctx.enter_context(tc.tile_pool(name="keep", bufs=1))
         psum = ctx.enter_context(tc.psum_pool(name="psum", bufs=1))
+
+        def mx(acc, w_code, w_scale, m_code, m_scale):
+            nc.tensor.matmul_mx(
+                out=acc,
+                lhsT=w_code.bitcast(FP8X4),
+                lhsT_scale=w_scale,
+                rhs=m_code.bitcast(FP8X4),
+                rhs_scale=m_scale,
+                start=True,
+                stop=True,
+            )
 
         offs_sb = keep.tile([P, S // 16], U16, name="offs_sb")
         la_sb = keep.tile([P, V // 16], U16, name="la_sb")
@@ -40,11 +53,11 @@ def tile_picked_tomein_none_p_kernel(tc, x_words, x_scales, w1, sz, w2, offs, la
         nc.vector.memset(scale_table[:].bitcast(I32), 0)
         w1_rows = w1.rearrange("(p j) c -> p j c", j=PACK)
         nc.sync.dma_start(offs_sb[:], offs)
-        nc.sync.dma_start(w1_raw[0][:], w1_rows[:, 0:2, :])
+        nc.sync.dma_start(word_table[:], x_words[0].rearrange("p n t -> p (n t)").bitcast(I32))
         for q in range(4):
             nc.sync.dma_start(scale_table[32 * q : 32 * q + 4, :].bitcast(I32), x_scales[0, 4 * q : 4 * q + 4, :].bitcast(I32))
+        nc.sync.dma_start(w1_raw[0][:], w1_rows[:, 0:2, :])
         nc.sync.dma_start(w1_raw[1][:], w1_rows[:, 2:4, :])
-        nc.sync.dma_start(word_table[:], x_words[0].rearrange("p n t -> p (n t)").bitcast(I32))
         nc.sync.dma_start(share_a[:], sz.rearrange("(p t) v -> p t v", t=PACK)[:, 0, :])
         nc.sync.dma_start(la_sb[:], la)
         nc.sync.dma_start(lb_sb[:], lb)
@@ -52,49 +65,58 @@ def tile_picked_tomein_none_p_kernel(tc, x_words, x_scales, w1, sz, w2, offs, la
 
         x_scale = keep.tile([P, S], U8, name="x_scale", align_bytes=64)
         nc.vector.tensor_copy(x_scale[:], scale_table[:].indirect(offs_sb[:]))
-
-        w1_bf = keep.tile([P, H * PACK], BF16, name="w1_bf", align_bytes=64)
-        w1_dst = w1_bf[:].rearrange("p (t m j) -> p m j t", t=PACK, j=PACK)
-        nc.scalar.copy(w1_dst[:, :, 0:2, :], w1_raw[0][:].rearrange("p j (m t) -> p m j t", t=PACK))
-        nc.vector.tensor_copy(w1_dst[:, :, 2:4, :], w1_raw[1][:].rearrange("p j (m t) -> p m j t", t=PACK))
-        w1_code = keep.tile([P, H], U32, name="w1_code", align_bytes=64)
-        w1_scale = keep.tile([P, H], U8, name="w1_scale", align_bytes=64)
-        nc.vector.quantize_mx(out=w1_code[:].bitcast(FP8X4), scales=w1_scale[:], in_=w1_bf[:])
-
         x_code = keep.tile([P, S], U32, name="x_code", align_bytes=64)
-        for h in range(2):
-            nc.vector.tensor_copy(
-                x_code[:, h * HALF : (h + 1) * HALF],
-                word_table[:].bitcast(U32).indirect(offs_sb[:, h * HALF // 16 : (h + 1) * HALF // 16]),
-            )
-        nc.vector.tensor_scalar(share_b[:], share_a[:], -1.0, 1.0, MULT, ADD)
+        nc.vector.tensor_copy(x_code[:], word_table[:].bitcast(U32).indirect(offs_sb[:]))
+
+        order = [2, 0, 1, 3]
+        w1_bf = [keep.tile([P, 2 * P * PACK], BF16, name=f"w1_bf{o}", align_bytes=64) for o in range(2)]
+        w1_code = [keep.tile([P, P], U32, name=f"w1_code{t}", align_bytes=64) for t in range(PACK)]
+        w1_scale = [keep.tile([P, P], U8, name=f"w1_scale{t}", align_bytes=64) for t in range(PACK)]
+        w1_src = [w1_raw[u][:].rearrange("p j (m e o) -> p o m j e", e=2, o=2) for u in range(2)]
+        w1_dst = [w1_bf[o][:].rearrange("p (e m j) -> p m j e", e=2, j=PACK) for o in range(2)]
+        for o in range(2):
+            nc.scalar.copy(w1_dst[o][:, :, 0:2, :], w1_src[0][:, o])
+        nc.scalar.copy(w1_dst[1][:, :, 2:4, :], w1_src[1][:, 1])
+        for t in order:
+            e, o = divmod(t, 2)
+            if o == 0:
+                nc.vector.tensor_copy(w1_dst[0][:, :, 2:4, e], w1_src[1][:, 0, :, :, e])
+            nc.vector.quantize_mx(out=w1_code[t][:].bitcast(FP8X4), scales=w1_scale[t][:], in_=w1_bf[o][:, e * S : (e + 1) * S])
 
         y = [keep.tile([P, S], F32, name=f"y{t}") for t in range(PACK)]
-        order = [2, 0, 1, 3]
-        pieces = [(order[0], 0, HALF), (order[1], 0, HALF), (order[0], HALF, S), (order[1], HALF, S), (order[2], 0, S), (order[3], 0, S)]
+        pieces = [(order[0], 0, HALF), (order[0], HALF, HALF + QUART), (order[0], HALF + QUART, S)] + [(t, 0, S) for t in order[1:]]
         for b, (t, lo, hi) in enumerate(pieces):
             acc = psum.tile([P, hi - lo], F32, name=f"acc_y{b}", tag=f"bank{b}")
-            nc.tensor.matmul_mx(
-                out=acc[:],
-                lhsT=w1_code[:, t * P : (t + 1) * P].bitcast(FP8X4),
-                lhsT_scale=w1_scale[:, t * P : (t + 1) * P],
-                rhs=x_code[:, lo:hi].bitcast(FP8X4),
-                rhs_scale=x_scale[:, lo:hi],
-                start=True,
-                stop=True,
-            )
-            nc.scalar.copy(y[t][:, lo:hi], acc[:])
+            mx(acc[:], w1_code[t][:], w1_scale[t][:], x_code[:, lo:hi], x_scale[:, lo:hi])
+            if hi - lo == QUART:
+                nc.vector.tensor_copy(y[t][:, lo:hi], acc[:])
+            else:
+                nc.scalar.copy(y[t][:, lo:hi], acc[:])
+            if b == 0:
+                nc.scalar.activation(share_b[:], share_a[:], COPY, scale=-1.0, bias=1.0)
 
-        w2_bf = keep.tile([P, N * PACK], BF16, name="w2_bf", align_bytes=64)
-        w2_dst = w2_bf[:].rearrange("p (c i j) -> p c j i", i=4, j=PACK)
-        w2_src = w2_raw[:].rearrange("p j (c i) -> p c j i", i=4)
-        for u in range(2):
-            nc.scalar.copy(w2_dst[:, u * 64 : (u + 1) * 64], w2_src[:, u * 64 : (u + 1) * 64])
-        w2_code = keep.tile([P, N], U32, name="w2_code", align_bytes=64)
-        w2_scale = keep.tile([P, N], U8, name="w2_scale", align_bytes=64)
+        groups = [(0, 1), (1, 2), (2, 4)]
+        w2_bf = [keep.tile([P, (hi - lo) * P, PACK], BF16, name=f"w2_bf{lo}", align_bytes=64) for lo, hi in groups]
 
-        part_a = [keep.tile([P, V], F32, name=f"part_a{t}") for t in range(PACK)]
-        part_b = [keep.tile([P, V], F32, name=f"part_b{t}") for t in range(PACK)]
+        def cast_w2(g):
+            lo, hi = groups[g]
+            nc.scalar.copy(w2_bf[g][:].rearrange("p (c i) j -> p c j i", i=4), w2_raw[:, :, lo * P : hi * P].rearrange("p j (c i) -> p c j i", i=4))
+
+        cast_w2(0)
+        w2_code = {}
+        w2_scale = {}
+
+        def quantise_w2(g, tag):
+            lo, hi = groups[g]
+            code = keep.tile([P, (hi - lo) * P], U32, name=f"w2_code{g}", tag=tag, align_bytes=64)
+            scale = keep.tile([P, (hi - lo) * P], U8, name=f"w2_scale{g}", align_bytes=64)
+            nc.vector.quantize_mx(out=code[:].bitcast(FP8X4), scales=scale[:], in_=w2_bf[g][:].rearrange("p c j -> p (c j)"))
+            for m in range(lo, hi):
+                w2_code[m] = code[:, (m - lo) * P : (m - lo + 1) * P]
+                w2_scale[m] = scale[:, (m - lo) * P : (m - lo + 1) * P]
+
+        part_a = [keep.tile([P, V], F32, name=f"part_a{t}", align_bytes=64) for t in range(PACK)]
+        part_b = [keep.tile([P, V], F32, name=f"part_b{t}", align_bytes=64) for t in range(PACK)]
         zs = {}
         zs_bf = [keep.tile([P, HALF, PACK], BF16, name=f"zs_bf{h}", align_bytes=64) for h in range(2)]
 
@@ -111,40 +133,49 @@ def tile_picked_tomein_none_p_kernel(tc, x_words, x_scales, w1, sz, w2, offs, la
         gather_b(order[0])
         for i, t in enumerate(order):
             last = i + 1 == PACK
-            zs[t] = keep.tile([P, S], F32, name=f"zs{t}", tag=f"zs{min(t, 2)}")
+            zs[t] = keep.tile([P, S], F32, name=f"zs{t}", align_bytes=64)
             if not last:
                 gather_a(order[i + 1])
             scatter(t, la_sb)
             if not last:
                 gather_b(order[i + 1])
-            else:
-                nc.vector.quantize_mx(out=w2_code[:].bitcast(FP8X4), scales=w2_scale[:], in_=w2_bf[:])
             scatter(t, lb_sb)
             if not last:
                 for h in range(2):
                     nc.scalar.copy(zs_bf[h][:, :, t], zs[t][:, h * HALF : (h + 1) * HALF])
+            if i == 0:
+                cast_w2(1)
+                cast_w2(2)
 
-        nc.vector.tensor_copy(zs_bf[0][:, :, PACK - 1], zs[PACK - 1][:, 0:HALF])
-        nc.scalar.copy(zs_bf[1][:, :, PACK - 1], zs[PACK - 1][:, HALF:S])
+        t = order[-1]
+        z_code = [keep.tile([P, HALF], U32, name=f"z_code{h}", align_bytes=64) for h in range(2)]
+        z_scale = [keep.tile([P, HALF], U8, name=f"z_scale{h}", align_bytes=64) for h in range(2)]
+
+        def lay(h, lo, hi):
+            nc.vector.tensor_copy(zs_bf[h][:, lo:hi, t], zs[t][:, h * HALF + lo : h * HALF + hi])
+
+        def quantise_z(h, lo, hi):
+            nc.vector.quantize_mx(out=z_code[h][:, lo:hi].bitcast(FP8X4), scales=z_scale[h][:, lo:hi], in_=zs_bf[h][:, lo:hi, :].rearrange("p c j -> p (c j)"))
+
+        quantise_w2(0, f"zs{order[0]}")
+        lay(0, 0, QUART)
+        lay(0, QUART, HALF)
+        nc.scalar.copy(zs_bf[1][:, :, t], zs[t][:, HALF:S])
+        quantise_z(0, 0, QUART)
+        quantise_z(0, QUART, HALF)
+        quantise_w2(1, f"part_a{t}")
+        quantise_w2(2, f"part_b{t}")
+        quantise_z(1, 0, HALF)
 
         for h in range(2):
-            z_code = keep.tile([P, HALF], U32, name=f"z_code{h}", align_bytes=64)
-            z_scale = keep.tile([P, HALF], U8, name=f"z_scale{h}", align_bytes=64)
-            nc.vector.quantize_mx(out=z_code[:].bitcast(FP8X4), scales=z_scale[:], in_=zs_bf[h][:].rearrange("p c j -> p (c j)"))
             for m in range(N // P):
                 b = h * (N // P) + m
                 acc = psum.tile([P, HALF], F32, name=f"acc_o{b}", tag=f"bank{b}")
-                nc.tensor.matmul_mx(
-                    out=acc[:],
-                    lhsT=w2_code[:, m * P : (m + 1) * P].bitcast(FP8X4),
-                    lhsT_scale=w2_scale[:, m * P : (m + 1) * P],
-                    rhs=z_code[:].bitcast(FP8X4),
-                    rhs_scale=z_scale[:],
-                    start=True,
-                    stop=True,
-                )
+                spans = [(0, QUART), (QUART, HALF)] if b == 0 else [(0, HALF)]
+                for lo, hi in spans:
+                    mx(acc[:, lo:hi], w2_code[m], w2_scale[m], z_code[h][:, lo:hi], z_scale[h][:, lo:hi])
                 res = keep.tile([P, HALF], F32, name=f"res{b}")
-                if b % 2 == 0:
+                if b in (3, 5, 7):
                     nc.vector.tensor_copy(res[:], acc[:])
                 else:
                     nc.scalar.copy(res[:], acc[:])

@@ -52,11 +52,11 @@ def tile_picked_tomein_none_p_kernel(tc, x_words, x_scales, w1, sz, w2, offs, la
 
         nc.vector.memset(scale_table[:].bitcast(I32), 0)
         w1_rows = w1.rearrange("(p j) c -> p j c", j=PACK)
+        nc.sync.dma_start(w1_raw[0][:], w1_rows[:, 0:2, :])
         nc.sync.dma_start(offs_sb[:], offs)
-        nc.sync.dma_start(word_table[:], x_words[0].rearrange("p n t -> p (n t)").bitcast(I32))
         for q in range(4):
             nc.sync.dma_start(scale_table[32 * q : 32 * q + 4, :].bitcast(I32), x_scales[0, 4 * q : 4 * q + 4, :].bitcast(I32))
-        nc.sync.dma_start(w1_raw[0][:], w1_rows[:, 0:2, :])
+        nc.sync.dma_start(word_table[:], x_words[0].rearrange("p n t -> p (n t)").bitcast(I32))
         nc.sync.dma_start(w1_raw[1][:], w1_rows[:, 2:4, :])
         nc.sync.dma_start(share_a[:], sz.rearrange("(p t) v -> p t v", t=PACK)[:, 0, :])
         nc.sync.dma_start(la_sb[:], la)

@@ -19,23 +19,28 @@ COPY = mybir.ActivationFunctionType.Copy
 
 P = 128
 PACK = 4
+BANKS = 8
 HALF = S // 2
-QUART = S // 4
+QUARTER = S // 4
+ROW_TILES = N // P
+
+PLANE_ORDER = [2, 0, 1, 3]
 
 
 def tile_picked_tomein_none_p_kernel(tc, x_words, x_scales, w1, sz, w2, offs, la, lb, out):
     nc = tc.nc
+    first_plane, last_plane = PLANE_ORDER[0], PLANE_ORDER[-1]
     with ExitStack() as ctx:
         keep = ctx.enter_context(tc.tile_pool(name="keep", bufs=1))
         psum = ctx.enter_context(tc.psum_pool(name="psum", bufs=1))
 
-        def mx(acc, w_code, w_scale, m_code, m_scale):
+        def product(acc, still_code, still_scale, moving_code, moving_scale):
             nc.tensor.matmul_mx(
                 out=acc,
-                lhsT=w_code.bitcast(FP8X4),
-                lhsT_scale=w_scale,
-                rhs=m_code.bitcast(FP8X4),
-                rhs_scale=m_scale,
+                lhsT=still_code.bitcast(FP8X4),
+                lhsT_scale=still_scale,
+                rhs=moving_code.bitcast(FP8X4),
+                rhs_scale=moving_scale,
                 start=True,
                 stop=True,
             )
@@ -54,8 +59,9 @@ def tile_picked_tomein_none_p_kernel(tc, x_words, x_scales, w1, sz, w2, offs, la
         w1_rows = w1.rearrange("(p j) c -> p j c", j=PACK)
         nc.sync.dma_start(w1_raw[0][:], w1_rows[:, 0:2, :])
         nc.sync.dma_start(offs_sb[:], offs)
-        for q in range(4):
-            nc.sync.dma_start(scale_table[32 * q : 32 * q + 4, :].bitcast(I32), x_scales[0, 4 * q : 4 * q + 4, :].bitcast(I32))
+        scale_rows = x_scales[0].bitcast(I32).rearrange("(q r) c -> r q c", r=4)
+        for r in range(4):
+            nc.sync.dma_start(scale_table[r:P:32, :].bitcast(I32), scale_rows[r])
         nc.sync.dma_start(word_table[:], x_words[0].rearrange("p n t -> p (n t)").bitcast(I32))
         nc.sync.dma_start(w1_raw[1][:], w1_rows[:, 2:4, :])
         nc.sync.dma_start(share_a[:], sz.rearrange("(p t) v -> p t v", t=PACK)[:, 0, :])
@@ -68,57 +74,68 @@ def tile_picked_tomein_none_p_kernel(tc, x_words, x_scales, w1, sz, w2, offs, la
         x_code = keep.tile([P, S], U32, name="x_code", align_bytes=64)
         nc.vector.tensor_copy(x_code[:], word_table[:].bitcast(U32).indirect(offs_sb[:]))
 
-        order = [2, 0, 1, 3]
+        even_planes, odd_planes = PLANE_ORDER[:2], PLANE_ORDER[2:]
         w1_bf = [keep.tile([P, 2 * P * PACK], BF16, name=f"w1_bf{o}", align_bytes=64) for o in range(2)]
-        w1_code = [keep.tile([P, P], U32, name=f"w1_code{t}", align_bytes=64) for t in range(PACK)]
-        w1_scale = [keep.tile([P, P], U8, name=f"w1_scale{t}", align_bytes=64) for t in range(PACK)]
         w1_src = [w1_raw[u][:].rearrange("p j (m e o) -> p o m j e", e=2, o=2) for u in range(2)]
         w1_dst = [w1_bf[o][:].rearrange("p (e m j) -> p m j e", e=2, j=PACK) for o in range(2)]
         for o in range(2):
             nc.scalar.copy(w1_dst[o][:, :, 0:2, :], w1_src[0][:, o])
+        nc.scalar.copy(w1_dst[0][:, P // 2 :, 2:4, first_plane // 2], w1_src[1][:, 0, P // 2 :, :, first_plane // 2])
         nc.scalar.copy(w1_dst[1][:, :, 2:4, :], w1_src[1][:, 1])
-        for t in order:
-            e, o = divmod(t, 2)
-            if o == 0:
-                nc.vector.tensor_copy(w1_dst[0][:, :, 2:4, e], w1_src[1][:, 0, :, :, e])
-            nc.vector.quantize_mx(out=w1_code[t][:].bitcast(FP8X4), scales=w1_scale[t][:], in_=w1_bf[o][:, e * S : (e + 1) * S])
+        w1_code = {}
+        w1_scale = {}
+        for t in even_planes:
+            e = t // 2
+            width = P // 2 if t == first_plane else P
+            nc.vector.tensor_copy(w1_dst[0][:, :width, 2:4, e], w1_src[1][:, 0, :width, :, e])
+            w1_code[t] = keep.tile([P, P], U32, name=f"w1_code{t}", align_bytes=64)[:]
+            w1_scale[t] = keep.tile([P, P], U8, name=f"w1_scale{t}", align_bytes=64)[:]
+            nc.vector.quantize_mx(out=w1_code[t].bitcast(FP8X4), scales=w1_scale[t], in_=w1_bf[0][:, e * P * PACK : (e + 1) * P * PACK])
 
         y = [keep.tile([P, S], F32, name=f"y{t}") for t in range(PACK)]
-        pieces = [(order[0], 0, HALF), (order[0], HALF, HALF + QUART), (order[0], HALF + QUART, S)] + [(t, 0, S) for t in order[1:]]
-        for b, (t, lo, hi) in enumerate(pieces):
-            acc = psum.tile([P, hi - lo], F32, name=f"acc_y{b}", tag=f"bank{b}")
-            mx(acc[:], w1_code[t][:], w1_scale[t][:], x_code[:, lo:hi], x_scale[:, lo:hi])
-            if hi - lo == QUART:
+
+        def make_y(bank, t, lo, hi):
+            acc = psum.tile([P, hi - lo], F32, name=f"acc_y{bank}", tag=f"bank{bank}")
+            product(acc[:], w1_code[t], w1_scale[t], x_code[:, lo:hi], x_scale[:, lo:hi])
+            if hi - lo == QUARTER:
                 nc.vector.tensor_copy(y[t][:, lo:hi], acc[:])
             else:
                 nc.scalar.copy(y[t][:, lo:hi], acc[:])
-            if b == 0:
-                nc.scalar.activation(share_b[:], share_a[:], COPY, scale=-1.0, bias=1.0)
 
-        groups = [(0, 1), (1, 2), (2, 4)]
-        w2_bf = [keep.tile([P, (hi - lo) * P, PACK], BF16, name=f"w2_bf{lo}", align_bytes=64) for lo, hi in groups]
+        make_y(0, first_plane, 0, HALF)
+        nc.scalar.activation(share_b[:], share_a[:], COPY, scale=-1.0, bias=1.0)
+        make_y(1, first_plane, HALF, HALF + QUARTER)
+        make_y(2, first_plane, HALF + QUARTER, S)
+        make_y(3, even_planes[1], 0, S)
+        odd_code = keep.tile([P, 2 * P], U32, name="odd_code", tag=f"w1_code{first_plane}", align_bytes=64)
+        odd_scale = keep.tile([P, 2 * P], U8, name="odd_scale", align_bytes=64)
+        nc.vector.quantize_mx(out=odd_code[:].bitcast(FP8X4), scales=odd_scale[:], in_=w1_bf[1][:])
+        for e, t in enumerate(odd_planes):
+            w1_code[t] = odd_code[:, e * P : (e + 1) * P]
+            w1_scale[t] = odd_scale[:, e * P : (e + 1) * P]
+            make_y(4 + e, t, 0, S)
 
-        def cast_w2(g):
-            lo, hi = groups[g]
-            nc.scalar.copy(w2_bf[g][:].rearrange("p (c i) j -> p c j i", i=4), w2_raw[:, :, lo * P : hi * P].rearrange("p j (c i) -> p c j i", i=4))
-
-        cast_w2(0)
+        w2_bf = [keep.tile([P, P, PACK], BF16, name=f"w2_bf{m}", align_bytes=64) for m in range(ROW_TILES)]
         w2_code = {}
         w2_scale = {}
 
-        def quantise_w2(g, tag):
-            lo, hi = groups[g]
-            code = keep.tile([P, (hi - lo) * P], U32, name=f"w2_code{g}", tag=tag, align_bytes=64)
-            scale = keep.tile([P, (hi - lo) * P], U8, name=f"w2_scale{g}", align_bytes=64)
-            nc.vector.quantize_mx(out=code[:].bitcast(FP8X4), scales=scale[:], in_=w2_bf[g][:].rearrange("p c j -> p (c j)"))
-            for m in range(lo, hi):
-                w2_code[m] = code[:, (m - lo) * P : (m - lo + 1) * P]
-                w2_scale[m] = scale[:, (m - lo) * P : (m - lo + 1) * P]
+        def cast_w2(m):
+            nc.scalar.copy(
+                w2_bf[m][:].rearrange("p (c i) j -> p c j i", i=4),
+                w2_raw[:, :, m * P : (m + 1) * P].rearrange("p j (c i) -> p c j i", i=4),
+            )
+
+        def quantise_w2(m, after):
+            w2_code[m] = keep.tile([P, P], U32, name=f"w2_code{m}", tag=after, align_bytes=64)
+            w2_scale[m] = keep.tile([P, P], U8, name=f"w2_scale{m}", align_bytes=64)
+            nc.vector.quantize_mx(out=w2_code[m][:].bitcast(FP8X4), scales=w2_scale[m][:], in_=w2_bf[m][:].rearrange("p c j -> p (c j)"))
+
+        cast_w2(0)
 
         part_a = [keep.tile([P, V], F32, name=f"part_a{t}", align_bytes=64) for t in range(PACK)]
         part_b = [keep.tile([P, V], F32, name=f"part_b{t}", align_bytes=64) for t in range(PACK)]
-        zs = {}
         zs_bf = [keep.tile([P, HALF, PACK], BF16, name=f"zs_bf{h}", align_bytes=64) for h in range(2)]
+        zs = {t: keep.tile([P, S], F32, name=f"zs{t}", align_bytes=64) for t in PLANE_ORDER}
 
         def gather_a(t):
             nc.vector.tensor_tensor(part_a[t][:], y[t][:].indirect(la_sb[:]), share_a[:], MULT)
@@ -129,54 +146,62 @@ def tile_picked_tomein_none_p_kernel(tc, x_words, x_scales, w1, sz, w2, offs, la
         def scatter(t, places):
             nc.vector.tensor_tensor(zs[t][:].indirect(places[:]), part_a[t][:], part_b[t][:], ADD)
 
-        gather_a(order[0])
-        gather_b(order[0])
-        for i, t in enumerate(order):
-            last = i + 1 == PACK
-            zs[t] = keep.tile([P, S], F32, name=f"zs{t}", align_bytes=64)
-            if not last:
-                gather_a(order[i + 1])
-            scatter(t, la_sb)
-            if not last:
-                gather_b(order[i + 1])
-            scatter(t, lb_sb)
-            if not last:
-                for h in range(2):
-                    nc.scalar.copy(zs_bf[h][:, :, t], zs[t][:, h * HALF : (h + 1) * HALF])
-            if i == 0:
-                cast_w2(1)
-                cast_w2(2)
+        def round_columns(t, h, lo, hi):
+            nc.scalar.copy(zs_bf[h][:, lo:hi, t], zs[t][:, h * HALF + lo : h * HALF + hi])
 
-        t = order[-1]
+        gather_a(first_plane)
+        gather_b(first_plane)
+        for t, following in zip(PLANE_ORDER, PLANE_ORDER[1:]):
+            gather_a(following)
+            scatter(t, la_sb)
+            gather_b(following)
+            scatter(t, lb_sb)
+            for h in range(2):
+                round_columns(t, h, 0, HALF)
+            if t == first_plane:
+                for m in range(1, ROW_TILES):
+                    cast_w2(m)
+        scatter(last_plane, la_sb)
+        scatter(last_plane, lb_sb)
+
         z_code = [keep.tile([P, HALF], U32, name=f"z_code{h}", align_bytes=64) for h in range(2)]
         z_scale = [keep.tile([P, HALF], U8, name=f"z_scale{h}", align_bytes=64) for h in range(2)]
+        quarters = [(0, QUARTER), (QUARTER, HALF)]
 
-        def lay(h, lo, hi):
-            nc.vector.tensor_copy(zs_bf[h][:, lo:hi, t], zs[t][:, h * HALF + lo : h * HALF + hi])
+        def quantise_zs(h, lo, hi):
+            nc.vector.quantize_mx(
+                out=z_code[h][:, lo:hi].bitcast(FP8X4), scales=z_scale[h][:, lo:hi], in_=zs_bf[h][:, lo:hi, :].rearrange("p c j -> p (c j)")
+            )
 
-        def quantise_z(h, lo, hi):
-            nc.vector.quantize_mx(out=z_code[h][:, lo:hi].bitcast(FP8X4), scales=z_scale[h][:, lo:hi], in_=zs_bf[h][:, lo:hi, :].rearrange("p c j -> p (c j)"))
+        quantise_w2(0, f"zs{first_plane}")
+        quantise_w2(1, "w2_bf0")
+        for lo, hi in quarters:
+            nc.vector.tensor_copy(zs_bf[0][:, lo:hi, last_plane], zs[last_plane][:, lo:hi])
+        for lo, hi in quarters:
+            round_columns(last_plane, 1, lo, hi)
+        for lo, hi in quarters:
+            quantise_zs(0, lo, hi)
+        quantise_zs(1, *quarters[0])
+        quantise_w2(2, "zs_bf0")
+        quantise_zs(1, *quarters[1])
+        quantise_w2(3, "zs_bf1")
 
-        quantise_w2(0, f"zs{order[0]}")
-        lay(0, 0, QUART)
-        lay(0, QUART, HALF)
-        nc.scalar.copy(zs_bf[1][:, :, t], zs[t][:, HALF:S])
-        quantise_z(0, 0, QUART)
-        quantise_z(0, QUART, HALF)
-        quantise_w2(1, f"part_a{t}")
-        quantise_w2(2, f"part_b{t}")
-        quantise_z(1, 0, HALF)
-
-        for h in range(2):
-            for m in range(N // P):
-                b = h * (N // P) + m
-                acc = psum.tile([P, HALF], F32, name=f"acc_o{b}", tag=f"bank{b}")
-                spans = [(0, QUART), (QUART, HALF)] if b == 0 else [(0, HALF)]
-                for lo, hi in spans:
-                    mx(acc[:, lo:hi], w2_code[m], w2_scale[m], z_code[h][:, lo:hi], z_scale[h][:, lo:hi])
-                res = keep.tile([P, HALF], F32, name=f"res{b}")
-                if b in (3, 5, 7):
-                    nc.vector.tensor_copy(res[:], acc[:])
-                else:
-                    nc.scalar.copy(res[:], acc[:])
-                nc.sync.dma_start(out[m * P : (m + 1) * P, h * HALF : (h + 1) * HALF], res[:])
+        res = [keep.tile([P, S], F32, name=f"res{m}") for m in range(ROW_TILES)]
+        scalar_alone, stored_by_halves = 3, 2
+        out_pieces = [(0, 0, lo, hi) for lo, hi in quarters] + [(m, 0, 0, HALF) for m in range(1, ROW_TILES - 1)]
+        out_pieces = out_pieces + [(m, 1, 0, HALF) for m in range(ROW_TILES - 1)] + [(ROW_TILES - 1, h, 0, HALF) for h in range(2)]
+        for n, (m, h, lo, hi) in enumerate(out_pieces):
+            acc = psum.tile([P, hi - lo], F32, name=f"acc_out{n}", tag=f"bank{n % BANKS}")
+            for c0, c1 in quarters if (m, h) == (0, 1) else [(lo, hi)]:
+                product(acc[:, c0 - lo : c1 - lo], w2_code[m][:], w2_scale[m][:], z_code[h][:, c0:c1], z_scale[h][:, c0:c1])
+            piece = res[m][:, h * HALF + lo : h * HALF + hi]
+            if n >= scalar_alone and (n - scalar_alone) % 2 == 0:
+                nc.vector.tensor_copy(piece, acc[:])
+            else:
+                nc.scalar.copy(piece, acc[:])
+            rows = slice(m * P, (m + 1) * P)
+            if m < stored_by_halves and hi == HALF:
+                cols = slice(h * HALF, (h + 1) * HALF)
+                nc.sync.dma_start(out[rows, cols], res[m][:, cols])
+            elif h == 1:
+                nc.sync.dma_start(out[rows, :], res[m][:])

@@ -48,29 +48,27 @@ def tile_picked_tomein_none_p_kernel(tc, x_words, x_scales, w1, sz, w2, offs, la
         offs_sb = keep.tile([P, S // 16], U16, name="offs_sb")
         la_sb = keep.tile([P, V // 16], U16, name="la_sb")
         lb_sb = keep.tile([P, V // 16], U16, name="lb_sb")
-        word_table = keep.tile([P, T], I32, name="word_table")
+        word_table = keep.tile([P, T], I32, name="word_table", tag="big")
         scale_table = keep.tile([P, T], U8, name="scale_table")
         w1_raw = [keep.tile([P, 2, H], F32, name=f"w1_raw{u}") for u in range(2)]
-        w2_raw = keep.tile([P, PACK, N], F32, name="w2_raw")
-        share_a = keep.tile([P, V], F32, name="share_a")
         share_b = keep.tile([P, V], F32, name="share_b")
 
         nc.vector.memset(scale_table[:].bitcast(I32), 0)
         w1_rows = w1.rearrange("(p j) c -> p j c", j=PACK)
         nc.sync.dma_start(w1_raw[0][:], w1_rows[:, 0:2, :])
         nc.sync.dma_start(offs_sb[:], offs)
-        scale_rows = x_scales[0].bitcast(I32).rearrange("(q r) c -> r q c", r=4)
-        for r in range(4):
-            nc.sync.dma_start(scale_table[r:P:32, :].bitcast(I32), scale_rows[r])
+        nc.sync.dma_start(scale_table[0:P:8, :].bitcast(I32), x_scales[0].bitcast(I32))
         nc.sync.dma_start(word_table[:], x_words[0].rearrange("p n t -> p (n t)").bitcast(I32))
         nc.sync.dma_start(w1_raw[1][:], w1_rows[:, 2:4, :])
-        nc.sync.dma_start(share_a[:], sz.rearrange("(p t) v -> p t v", t=PACK)[:, 0, :])
         nc.sync.dma_start(la_sb[:], la)
         nc.sync.dma_start(lb_sb[:], lb)
-        nc.sync.dma_start(w2_raw[:], w2.rearrange("(p j) c -> p j c", j=PACK))
 
+        picked = keep.tile([P, S], U8, name="picked", align_bytes=64)
+        nc.vector.tensor_copy(picked[:], scale_table[:].indirect(offs_sb[:]))
         x_scale = keep.tile([P, S], U8, name="x_scale", align_bytes=64)
-        nc.vector.tensor_copy(x_scale[:], scale_table[:].indirect(offs_sb[:]))
+        nc.vector.memset(x_scale[:].bitcast(I32), 0)
+        for r in range(4):
+            nc.sync.dma_start(x_scale[r:P:32, :].bitcast(I32), picked[8 * r : P : 32, :].bitcast(I32))
         x_code = keep.tile([P, S], U32, name="x_code", align_bytes=64)
         nc.vector.tensor_copy(x_code[:], word_table[:].bitcast(U32).indirect(offs_sb[:]))
 
@@ -80,6 +78,10 @@ def tile_picked_tomein_none_p_kernel(tc, x_words, x_scales, w1, sz, w2, offs, la
         w1_dst = [w1_bf[o][:].rearrange("p (e m j) -> p m j e", e=2, j=PACK) for o in range(2)]
         for o in range(2):
             nc.scalar.copy(w1_dst[o][:, :, 0:2, :], w1_src[0][:, o])
+        share_a = keep.tile([P, V], F32, name="share_a", tag="w1_raw0")
+        nc.sync.dma_start(share_a[:], sz.rearrange("(p t) v -> p t v", t=PACK)[:, 0, :])
+        w2_raw = keep.tile([P, PACK, N], F32, name="w2_raw", tag="big")
+        nc.sync.dma_start(w2_raw[:], w2.rearrange("(p j) c -> p j c", j=PACK))
         nc.scalar.copy(w1_dst[0][:, P // 2 :, 2:4, first_plane // 2], w1_src[1][:, 0, P // 2 :, :, first_plane // 2])
         nc.scalar.copy(w1_dst[1][:, :, 2:4, :], w1_src[1][:, 1])
         w1_code = {}

@@ -96,26 +96,29 @@ def tile_picked_tomein_none_p_kernel(tc, x_words, x_scales, w1, sz, w2, offs, la
 
         y = [keep.tile([P, S], F32, name=f"y{t}") for t in range(PACK)]
 
-        def make_y(bank, t, lo, hi):
-            acc = psum.tile([P, hi - lo], F32, name=f"acc_y{bank}", tag=f"bank{bank}")
+        def make_y(bank, t, lo, hi, on_vector=False):
+            acc = psum.tile([P, hi - lo], F32, name=f"acc_y{bank}", tag=f"bank{bank % BANKS}")
             product(acc[:], w1_code[t], w1_scale[t], x_code[:, lo:hi], x_scale[:, lo:hi])
-            if hi - lo == QUARTER:
+            if on_vector:
                 nc.vector.tensor_copy(y[t][:, lo:hi], acc[:])
             else:
                 nc.scalar.copy(y[t][:, lo:hi], acc[:])
 
-        make_y(0, first_plane, 0, HALF)
+        make_y(0, first_plane, 0, QUARTER)
+        make_y(1, first_plane, QUARTER, HALF, True)
+        make_y(2, first_plane, HALF, HALF + QUARTER)
+        make_y(3, first_plane, HALF + QUARTER, S, True)
         nc.scalar.activation(share_b[:], share_a[:], COPY, scale=-1.0, bias=1.0)
-        make_y(1, first_plane, HALF, HALF + QUARTER)
-        make_y(2, first_plane, HALF + QUARTER, S)
-        make_y(3, even_planes[1], 0, S)
+        make_y(4, even_planes[1], 0, HALF)
+        make_y(5, even_planes[1], HALF, S)
         odd_code = keep.tile([P, 2 * P], U32, name="odd_code", tag=f"w1_code{first_plane}", align_bytes=64)
         odd_scale = keep.tile([P, 2 * P], U8, name="odd_scale", align_bytes=64)
         nc.vector.quantize_mx(out=odd_code[:].bitcast(FP8X4), scales=odd_scale[:], in_=w1_bf[1][:])
         for e, t in enumerate(odd_planes):
             w1_code[t] = odd_code[:, e * P : (e + 1) * P]
             w1_scale[t] = odd_scale[:, e * P : (e + 1) * P]
-            make_y(4 + e, t, 0, S)
+            make_y(6 + 2 * e, t, 0, HALF)
+            make_y(7 + 2 * e, t, HALF, S)
 
         w2_bf = [keep.tile([P, P, PACK], BF16, name=f"w2_bf{m}", align_bytes=64) for m in range(ROW_TILES)]
         w2_code = {}
@@ -176,6 +179,9 @@ def tile_picked_tomein_none_p_kernel(tc, x_words, x_scales, w1, sz, w2, offs, la
             )
 
         quantise_w2(0, f"zs{first_plane}")
+        for u in range(2):
+            idle = psum.tile([P, S], F32, name=f"idle{u}", tag=f"bank{BANKS - 1 - u}")
+            product(idle[:], w2_code[0][:], w2_scale[0][:], x_code[:], x_scale[:])
         quantise_w2(1, "w2_bf0")
         for lo, hi in quarters:
             nc.vector.tensor_copy(zs_bf[0][:, lo:hi, last_plane], zs[last_plane][:, lo:hi])

@@ -104,10 +104,10 @@ def tile_picked_tomein_none_p_kernel(tc, x_words, x_scales, w1, sz, w2, offs, la
             else:
                 nc.scalar.copy(y[t][:, lo:hi], acc[:])
 
-        make_y(0, first_plane, 0, QUARTER)
-        make_y(1, first_plane, QUARTER, HALF, True)
-        make_y(2, first_plane, HALF, HALF + QUARTER)
-        make_y(3, first_plane, HALF + QUARTER, S, True)
+        make_y(0, first_plane, 0, QUARTER, True)
+        make_y(1, first_plane, QUARTER, HALF)
+        make_y(2, first_plane, HALF, HALF + QUARTER, True)
+        make_y(3, first_plane, HALF + QUARTER, S)
         nc.scalar.activation(share_b[:], share_a[:], COPY, scale=-1.0, bias=1.0)
         make_y(4, even_planes[1], 0, HALF)
         make_y(5, even_planes[1], HALF, S)
@@ -120,22 +120,26 @@ def tile_picked_tomein_none_p_kernel(tc, x_words, x_scales, w1, sz, w2, offs, la
             make_y(6 + 2 * e, t, 0, HALF)
             make_y(7 + 2 * e, t, HALF, S)
 
-        w2_bf = [keep.tile([P, P, PACK], BF16, name=f"w2_bf{m}", align_bytes=64) for m in range(ROW_TILES)]
+        w2_bf = [keep.tile([P, 2 * P, PACK], BF16, name=f"w2_bf{u}", align_bytes=64) for u in range(2)]
         w2_code = {}
         w2_scale = {}
 
         def cast_w2(m):
             nc.scalar.copy(
-                w2_bf[m][:].rearrange("p (c i) j -> p c j i", i=4),
+                w2_bf[m // 2][:, m % 2 * P : (m % 2 + 1) * P, :].rearrange("p (c i) j -> p c j i", i=4),
                 w2_raw[:, :, m * P : (m + 1) * P].rearrange("p j (c i) -> p c j i", i=4),
             )
 
-        def quantise_w2(m, after):
-            w2_code[m] = keep.tile([P, P], U32, name=f"w2_code{m}", tag=after, align_bytes=64)
-            w2_scale[m] = keep.tile([P, P], U8, name=f"w2_scale{m}", align_bytes=64)
-            nc.vector.quantize_mx(out=w2_code[m][:].bitcast(FP8X4), scales=w2_scale[m][:], in_=w2_bf[m][:].rearrange("p c j -> p (c j)"))
+        def quantise_w2(u, after):
+            code = keep.tile([P, 2 * P], U32, name=f"w2_code{u}", tag=after, align_bytes=64)
+            scale = keep.tile([P, 2 * P], U8, name=f"w2_scale{u}", align_bytes=64)
+            nc.vector.quantize_mx(out=code[:].bitcast(FP8X4), scales=scale[:], in_=w2_bf[u][:].rearrange("p c j -> p (c j)"))
+            for e in range(2):
+                w2_code[2 * u + e] = code[:, e * P : (e + 1) * P]
+                w2_scale[2 * u + e] = scale[:, e * P : (e + 1) * P]
 
         cast_w2(0)
+        cast_w2(1)
 
         part_a = [keep.tile([P, V], F32, name=f"part_a{t}", align_bytes=64) for t in range(PACK)]
         part_b = [keep.tile([P, V], F32, name=f"part_b{t}", align_bytes=64) for t in range(PACK)]
@@ -164,7 +168,7 @@ def tile_picked_tomein_none_p_kernel(tc, x_words, x_scales, w1, sz, w2, offs, la
             for h in range(2):
                 round_columns(t, h, 0, HALF)
             if t == first_plane:
-                for m in range(1, ROW_TILES):
+                for m in range(2, ROW_TILES):
                     cast_w2(m)
         scatter(last_plane, la_sb)
         scatter(last_plane, lb_sb)
@@ -181,7 +185,7 @@ def tile_picked_tomein_none_p_kernel(tc, x_words, x_scales, w1, sz, w2, offs, la
         quantise_w2(0, f"zs{first_plane}")
         for u in range(2):
             idle = psum.tile([P, S], F32, name=f"idle{u}", tag=f"bank{BANKS - 1 - u}")
-            product(idle[:], w2_code[0][:], w2_scale[0][:], x_code[:], x_scale[:])
+            product(idle[:], w2_code[0], w2_scale[0], x_code[:], x_scale[:])
         quantise_w2(1, "w2_bf0")
         for lo, hi in quarters:
             nc.vector.tensor_copy(zs_bf[0][:, lo:hi, last_plane], zs[last_plane][:, lo:hi])
@@ -190,9 +194,7 @@ def tile_picked_tomein_none_p_kernel(tc, x_words, x_scales, w1, sz, w2, offs, la
         for lo, hi in quarters:
             quantise_zs(0, lo, hi)
         quantise_zs(1, *quarters[0])
-        quantise_w2(2, "zs_bf0")
         quantise_zs(1, *quarters[1])
-        quantise_w2(3, "zs_bf1")
 
         res = [keep.tile([P, S], F32, name=f"res{m}") for m in range(ROW_TILES)]
         scalar_alone, stored_by_halves = 3, 2
@@ -201,7 +203,7 @@ def tile_picked_tomein_none_p_kernel(tc, x_words, x_scales, w1, sz, w2, offs, la
         for n, (m, h, lo, hi) in enumerate(out_pieces):
             acc = psum.tile([P, hi - lo], F32, name=f"acc_out{n}", tag=f"bank{n % BANKS}")
             for c0, c1 in quarters if (m, h) == (0, 1) else [(lo, hi)]:
-                product(acc[:, c0 - lo : c1 - lo], w2_code[m][:], w2_scale[m][:], z_code[h][:, c0:c1], z_scale[h][:, c0:c1])
+                product(acc[:, c0 - lo : c1 - lo], w2_code[m], w2_scale[m], z_code[h][:, c0:c1], z_scale[h][:, c0:c1])
             piece = res[m][:, h * HALF + lo : h * HALF + hi]
             if n >= scalar_alone and (n - scalar_alone) % 2 == 0:
                 nc.vector.tensor_copy(piece, acc[:])

@@ -189,8 +189,9 @@ def tile_picked_tomein_none_p_kernel(tc, x_words, x_scales, w1, sz, w2, offs, la
         quantise_w2(1, "w2_bf0")
         for lo, hi in quarters:
             nc.vector.tensor_copy(zs_bf[0][:, lo:hi, last_plane], zs[last_plane][:, lo:hi])
-        for lo, hi in quarters:
-            round_columns(last_plane, 1, lo, hi)
+        nc.vector.tensor_copy(zs_bf[1][:, 0:96, last_plane], zs[last_plane][:, HALF : HALF + 96])
+        round_columns(last_plane, 1, 96, QUARTER)
+        round_columns(last_plane, 1, QUARTER, HALF)
         for lo, hi in quarters:
             quantise_zs(0, lo, hi)
         quantise_zs(1, *quarters[0])

@@ -198,7 +198,7 @@ def tile_picked_tomein_none_p_kernel(tc, x_words, x_scales, w1, sz, w2, offs, la
         quantise_zs(1, *quarters[1])
 
         res = [keep.tile([P, S], F32, name=f"res{m}") for m in range(ROW_TILES)]
-        scalar_alone, stored_by_halves = 3, 2
+        scalar_alone, stored_by_halves = 3, 4
         out_pieces = [(0, 0, lo, hi) for lo, hi in quarters] + [(m, 0, 0, HALF) for m in range(1, ROW_TILES - 1)]
         out_pieces = out_pieces + [(m, 1, 0, HALF) for m in range(ROW_TILES - 1)] + [(ROW_TILES - 1, h, 0, HALF) for h in range(2)]
         for n, (m, h, lo, hi) in enumerate(out_pieces):

@@ -50,16 +50,16 @@ def tile_picked_tomein_none_p_kernel(tc, x_words, x_scales, w1, sz, w2, offs, la
         lb_sb = keep.tile([P, V // 16], U16, name="lb_sb")
         word_table = keep.tile([P, T], I32, name="word_table", tag="big")
         scale_table = keep.tile([P, T], U8, name="scale_table")
-        w1_raw = [keep.tile([P, 2, H], F32, name=f"w1_raw{u}") for u in range(2)]
+        w1_raw = keep.tile([P, PACK * H], F32, name="w1_raw")
         share_b = keep.tile([P, V], F32, name="share_b")
 
         nc.vector.memset(scale_table[:].bitcast(I32), 0)
-        w1_rows = w1.rearrange("(p j) c -> p j c", j=PACK)
-        nc.sync.dma_start(w1_raw[0][:], w1_rows[:, 0:2, :])
+        w1_rows = w1.rearrange("(p j) c -> p (j c)", j=PACK)
+        nc.sync.dma_start(w1_raw[:, 0 : 2 * H], w1_rows[:, 0 : 2 * H])
         nc.sync.dma_start(offs_sb[:], offs)
         nc.sync.dma_start(scale_table[0:P:8, :].bitcast(I32), x_scales[0].bitcast(I32))
         nc.sync.dma_start(word_table[:], x_words[0].rearrange("p n t -> p (n t)").bitcast(I32))
-        nc.sync.dma_start(w1_raw[1][:], w1_rows[:, 2:4, :])
+        nc.sync.dma_start(w1_raw[:, 2 * H : 4 * H], w1_rows[:, 2 * H : 4 * H])
         nc.sync.dma_start(la_sb[:], la)
         nc.sync.dma_start(lb_sb[:], lb)
 
@@ -73,26 +73,28 @@ def tile_picked_tomein_none_p_kernel(tc, x_words, x_scales, w1, sz, w2, offs, la
         nc.vector.tensor_copy(x_code[:], word_table[:].bitcast(U32).indirect(offs_sb[:]))
 
         even_planes, odd_planes = PLANE_ORDER[:2], PLANE_ORDER[2:]
-        w1_bf = [keep.tile([P, 2 * P * PACK], BF16, name=f"w1_bf{o}", align_bytes=64) for o in range(2)]
-        w1_src = [w1_raw[u][:].rearrange("p j (m e o) -> p o m j e", e=2, o=2) for u in range(2)]
-        w1_dst = [w1_bf[o][:].rearrange("p (e m j) -> p m j e", e=2, j=PACK) for o in range(2)]
-        for o in range(2):
-            nc.scalar.copy(w1_dst[o][:, :, 0:2, :], w1_src[0][:, o])
-        share_a = keep.tile([P, V], F32, name="share_a", tag="w1_raw0")
+        w1_bf = {t: keep.tile([P, P, PACK], BF16, name=f"w1_bf{t}", align_bytes=64) for t in even_planes}
+        w1_src = [w1_raw[:, 2 * u * H : 2 * (u + 1) * H].rearrange("p (j m t) -> p t m j", j=2, t=PACK) for u in range(2)]
+        for t in even_planes:
+            nc.scalar.copy(w1_bf[t][:, :, 0:2], w1_src[0][:, t])
+        share_a = keep.tile([P, V], F32, name="share_a", tag="scale_table")
         nc.sync.dma_start(share_a[:], sz.rearrange("(p t) v -> p t v", t=PACK)[:, 0, :])
         w2_raw = keep.tile([P, PACK, N], F32, name="w2_raw", tag="big")
         nc.sync.dma_start(w2_raw[:], w2.rearrange("(p j) c -> p j c", j=PACK))
-        nc.scalar.copy(w1_dst[0][:, P // 2 :, 2:4, first_plane // 2], w1_src[1][:, 0, P // 2 :, :, first_plane // 2])
-        nc.scalar.copy(w1_dst[1][:, :, 2:4, :], w1_src[1][:, 1])
+        nc.scalar.copy(w1_bf[first_plane][:, 80:, 2:4], w1_src[1][:, first_plane, 80:, :])
         w1_code = {}
         w1_scale = {}
         for t in even_planes:
-            e = t // 2
-            width = P // 2 if t == first_plane else P
-            nc.vector.tensor_copy(w1_dst[0][:, :width, 2:4, e], w1_src[1][:, 0, :width, :, e])
+            width = 80 if t == first_plane else P
+            nc.vector.tensor_copy(w1_bf[t][:, :width, 2:4], w1_src[1][:, t, :width, :])
             w1_code[t] = keep.tile([P, P], U32, name=f"w1_code{t}", align_bytes=64)[:]
             w1_scale[t] = keep.tile([P, P], U8, name=f"w1_scale{t}", align_bytes=64)[:]
-            nc.vector.quantize_mx(out=w1_code[t].bitcast(FP8X4), scales=w1_scale[t], in_=w1_bf[0][:, e * P * PACK : (e + 1) * P * PACK])
+            nc.vector.quantize_mx(out=w1_code[t].bitcast(FP8X4), scales=w1_scale[t], in_=w1_bf[t][:].rearrange("p m j -> p (m j)"))
+        odd_bf = keep.tile([P, 2 * P * PACK], BF16, name="odd_bf", tag=f"w1_bf{first_plane}", align_bytes=64)
+        nc.vector.tensor_copy(
+            odd_bf[:].rearrange("p (e m j) -> p m j e", e=2, j=PACK),
+            w1_raw[:].rearrange("p (j m e o) -> p o m j e", j=PACK, e=2, o=2)[:, 1],
+        )
 
         y = [keep.tile([P, S], F32, name=f"y{t}") for t in range(PACK)]
 
@@ -104,16 +106,16 @@ def tile_picked_tomein_none_p_kernel(tc, x_words, x_scales, w1, sz, w2, offs, la
             else:
                 nc.scalar.copy(y[t][:, lo:hi], acc[:])
 
-        make_y(0, first_plane, 0, QUARTER, True)
+        make_y(0, first_plane, 0, QUARTER)
         make_y(1, first_plane, QUARTER, HALF)
-        make_y(2, first_plane, HALF, HALF + QUARTER, True)
+        make_y(2, first_plane, HALF, HALF + QUARTER)
         make_y(3, first_plane, HALF + QUARTER, S)
         nc.scalar.activation(share_b[:], share_a[:], COPY, scale=-1.0, bias=1.0)
         make_y(4, even_planes[1], 0, HALF)
         make_y(5, even_planes[1], HALF, S)
         odd_code = keep.tile([P, 2 * P], U32, name="odd_code", tag=f"w1_code{first_plane}", align_bytes=64)
         odd_scale = keep.tile([P, 2 * P], U8, name="odd_scale", align_bytes=64)
-        nc.vector.quantize_mx(out=odd_code[:].bitcast(FP8X4), scales=odd_scale[:], in_=w1_bf[1][:])
+        nc.vector.quantize_mx(out=odd_code[:].bitcast(FP8X4), scales=odd_scale[:], in_=odd_bf[:])
         for e, t in enumerate(odd_planes):
             w1_code[t] = odd_code[:, e * P : (e + 1) * P]
             w1_scale[t] = odd_scale[:, e * P : (e + 1) * P]

@@ -100,7 +100,8 @@ def tile_picked_tomein_none_p_kernel(tc, x_words, x_scales, w1, sz, w2, offs, la
 
         def make_y(bank, t, lo, hi, on_vector=False):
             acc = psum.tile([P, hi - lo], F32, name=f"acc_y{bank}", tag=f"bank{bank % BANKS}")
-            product(acc[:], w1_code[t], w1_scale[t], x_code[:, lo:hi], x_scale[:, lo:hi])
+            for c0 in range(lo, hi, QUARTER):
+                product(acc[:, c0 - lo : c0 - lo + QUARTER], w1_code[t], w1_scale[t], x_code[:, c0 : c0 + QUARTER], x_scale[:, c0 : c0 + QUARTER])
             if on_vector:
                 nc.vector.tensor_copy(y[t][:, lo:hi], acc[:])
             else:
@@ -185,9 +186,9 @@ def tile_picked_tomein_none_p_kernel(tc, x_words, x_scales, w1, sz, w2, offs, la
             )
 
         quantise_w2(0, f"zs{first_plane}")
-        for u in range(2):
-            idle = psum.tile([P, S], F32, name=f"idle{u}", tag=f"bank{BANKS - 1 - u}")
-            product(idle[:], w2_code[0], w2_scale[0], x_code[:], x_scale[:])
+        for u in range(3):
+            idle = psum.tile([P // 2, S], F32, name=f"idle{u}", tag=f"bank{BANKS - 1 - u}")
+            product(idle[:], w2_code[0][:, 0 : P // 2], w2_scale[0][:, 0 : P // 2], x_code[:], x_scale[:])
         quantise_w2(1, "w2_bf0")
         for lo, hi in quarters:
             nc.vector.tensor_copy(zs_bf[0][:, lo:hi, last_plane], zs[last_plane][:, lo:hi])
@@ -205,7 +206,7 @@ def tile_picked_tomein_none_p_kernel(tc, x_words, x_scales, w1, sz, w2, offs, la
         out_pieces = out_pieces + [(m, 1, 0, HALF) for m in range(ROW_TILES - 1)] + [(ROW_TILES - 1, h, 0, HALF) for h in range(2)]
         for n, (m, h, lo, hi) in enumerate(out_pieces):
             acc = psum.tile([P, hi - lo], F32, name=f"acc_out{n}", tag=f"bank{n % BANKS}")
-            for c0, c1 in quarters if (m, h) == (0, 1) else [(lo, hi)]:
+            for c0, c1 in quarters if m < ROW_TILES - 1 and hi - lo == HALF else [(lo, hi)]:
                 product(acc[:, c0 - lo : c1 - lo], w2_code[m], w2_scale[m], z_code[h][:, c0:c1], z_scale[h][:, c0:c1])
             piece = res[m][:, h * HALF + lo : h * HALF + hi]
             if n >= scalar_alone and (n - scalar_alone) % 2 == 0:

@@ -192,9 +192,8 @@ def tile_picked_tomein_none_p_kernel(tc, x_words, x_scales, w1, sz, w2, offs, la
         quantise_w2(1, "w2_bf0")
         for lo, hi in quarters:
             nc.vector.tensor_copy(zs_bf[0][:, lo:hi, last_plane], zs[last_plane][:, lo:hi])
-        nc.vector.tensor_copy(zs_bf[1][:, 0:96, last_plane], zs[last_plane][:, HALF : HALF + 96])
-        round_columns(last_plane, 1, 96, QUARTER)
-        round_columns(last_plane, 1, QUARTER, HALF)
+        nc.vector.tensor_copy(zs_bf[1][:, 0:48, last_plane], zs[last_plane][:, HALF : HALF + 48])
+        round_columns(last_plane, 1, 48, HALF)
         for lo, hi in quarters:
             quantise_zs(0, lo, hi)
         quantise_zs(1, *quarters[0])

@@ -51,7 +51,6 @@ def tile_picked_tomein_none_p_kernel(tc, x_words, x_scales, w1, sz, w2, offs, la
         word_table = keep.tile([P, T], I32, name="word_table", tag="big")
         scale_table = keep.tile([P, T], U8, name="scale_table")
         w1_raw = keep.tile([P, PACK * H], F32, name="w1_raw")
-        share_b = keep.tile([P, V], F32, name="share_b")
 
         nc.vector.memset(scale_table[:].bitcast(I32), 0)
         w1_rows = w1.rearrange("(p j) c -> p (j c)", j=PACK)
@@ -77,8 +76,8 @@ def tile_picked_tomein_none_p_kernel(tc, x_words, x_scales, w1, sz, w2, offs, la
         w1_src = [w1_raw[:, 2 * u * H : 2 * (u + 1) * H].rearrange("p (j m t) -> p t m j", j=2, t=PACK) for u in range(2)]
         for t in even_planes:
             nc.scalar.copy(w1_bf[t][:, :, 0:2], w1_src[0][:, t])
-        share_a = keep.tile([P, V], F32, name="share_a", tag="scale_table")
-        nc.sync.dma_start(share_a[:], sz.rearrange("(p t) v -> p t v", t=PACK)[:, 0, :])
+        share = keep.tile([P, 2 * V], F32, name="share", tag="scale_table")
+        nc.sync.dma_start(share[:, 0:V], sz.rearrange("(p t) v -> p t v", t=PACK)[:, 0, :])
         w2_raw = keep.tile([P, PACK, N], F32, name="w2_raw", tag="big")
         nc.sync.dma_start(w2_raw[:], w2.rearrange("(p j) c -> p j c", j=PACK))
         nc.scalar.copy(w1_bf[first_plane][:, 80:, 2:4], w1_src[1][:, first_plane, 80:, :])
@@ -96,7 +95,7 @@ def tile_picked_tomein_none_p_kernel(tc, x_words, x_scales, w1, sz, w2, offs, la
             w1_raw[:].rearrange("p (j m e o) -> p o m j e", j=PACK, e=2, o=2)[:, 1],
         )
 
-        y = [keep.tile([P, S], F32, name=f"y{t}") for t in range(PACK)]
+        y = [keep.tile([P, S], F32, name=f"y{t}", align_bytes=64) for t in range(PACK)]
 
         def make_y(bank, t, lo, hi, on_vector=False):
             acc = psum.tile([P, hi - lo], F32, name=f"acc_y{bank}", tag=f"bank{bank % BANKS}")
@@ -107,13 +106,23 @@ def tile_picked_tomein_none_p_kernel(tc, x_words, x_scales, w1, sz, w2, offs, la
             else:
                 nc.scalar.copy(y[t][:, lo:hi], acc[:])
 
+        pair = {t: keep.tile([P, 2 * V], F32, name=f"pair{t}", align_bytes=64) for t in PLANE_ORDER}
+        terms = {t: keep.tile([P, 2 * V], F32, name=f"terms{t}", align_bytes=64) for t in PLANE_ORDER}
+
+        def fetch(t, side):
+            places = (la_sb, lb_sb)[side]
+            nc.scalar.activation(pair[t][:, side * V : (side + 1) * V], y[t][:].indirect(places[:]), COPY)
+
+        nc.scalar.activation(share[:, V:], share[:, 0:V], COPY, scale=-1.0, bias=1.0)
         make_y(0, first_plane, 0, QUARTER)
         make_y(1, first_plane, QUARTER, HALF)
         make_y(2, first_plane, HALF, HALF + QUARTER)
         make_y(3, first_plane, HALF + QUARTER, S)
-        nc.scalar.activation(share_b[:], share_a[:], COPY, scale=-1.0, bias=1.0)
+        fetch(first_plane, 1)
         make_y(4, even_planes[1], 0, HALF)
         make_y(5, even_planes[1], HALF, S)
+        fetch(even_planes[1], 0)
+        fetch(even_planes[1], 1)
         odd_code = keep.tile([P, 2 * P], U32, name="odd_code", tag=f"w1_code{first_plane}", align_bytes=64)
         odd_scale = keep.tile([P, 2 * P], U8, name="odd_scale", align_bytes=64)
         nc.vector.quantize_mx(out=odd_code[:].bitcast(FP8X4), scales=odd_scale[:], in_=odd_bf[:])
@@ -122,6 +131,8 @@ def tile_picked_tomein_none_p_kernel(tc, x_words, x_scales, w1, sz, w2, offs, la
             w1_scale[t] = odd_scale[:, e * P : (e + 1) * P]
             make_y(6 + 2 * e, t, 0, HALF)
             make_y(7 + 2 * e, t, HALF, S)
+            fetch(t, 0)
+            fetch(t, 1)
 
         w2_bf = [keep.tile([P, 2 * P, PACK], BF16, name=f"w2_bf{u}", align_bytes=64) for u in range(2)]
         w2_code = {}
@@ -133,9 +144,9 @@ def tile_picked_tomein_none_p_kernel(tc, x_words, x_scales, w1, sz, w2, offs, la
                 w2_raw[:, :, m * P : (m + 1) * P].rearrange("p j (c i) -> p c j i", i=4),
             )
 
-        def quantise_w2(u, after):
+        def quantise_w2(u, after, scale_after):
             code = keep.tile([P, 2 * P], U32, name=f"w2_code{u}", tag=after, align_bytes=64)
-            scale = keep.tile([P, 2 * P], U8, name=f"w2_scale{u}", align_bytes=64)
+            scale = keep.tile([P, 2 * P], U8, name=f"w2_scale{u}", tag=scale_after, align_bytes=64)
             nc.vector.quantize_mx(out=code[:].bitcast(FP8X4), scales=scale[:], in_=w2_bf[u][:].rearrange("p c j -> p (c j)"))
             for e in range(2):
                 w2_code[2 * u + e] = code[:, e * P : (e + 1) * P]
@@ -144,35 +155,39 @@ def tile_picked_tomein_none_p_kernel(tc, x_words, x_scales, w1, sz, w2, offs, la
         cast_w2(0)
         cast_w2(1)
 
-        part_a = [keep.tile([P, V], F32, name=f"part_a{t}", align_bytes=64) for t in range(PACK)]
-        part_b = [keep.tile([P, V], F32, name=f"part_b{t}", align_bytes=64) for t in range(PACK)]
-        zs_bf = [keep.tile([P, HALF, PACK], BF16, name=f"zs_bf{h}", align_bytes=64) for h in range(2)]
-        zs = {t: keep.tile([P, S], F32, name=f"zs{t}", align_bytes=64) for t in PLANE_ORDER}
+        zs_bf = [keep.tile([P, HALF, PACK], BF16, name=f"zs_bf{h}", tag=f"y{PLANE_ORDER[-1 - h]}", align_bytes=64) for h in range(2)]
+        zs = {}
 
-        def gather_a(t):
-            nc.vector.tensor_tensor(part_a[t][:], y[t][:].indirect(la_sb[:]), share_a[:], MULT)
+        mix = {t: keep.tile([P, V], F32, name=f"mix{t}", align_bytes=64) for t in PLANE_ORDER}
 
-        def gather_b(t):
-            nc.vector.tensor_tensor(part_b[t][:], y[t][:].indirect(lb_sb[:]), share_b[:], MULT)
+        def weigh(engine, t, lo):
+            engine.tensor_tensor(terms[t][:, lo:], pair[t][:, lo:], share[:, lo:], MULT)
+
+        def add_terms(engine, t):
+            engine.tensor_tensor(mix[t][:], terms[t][:, 0:V], terms[t][:, V:], ADD)
 
         def scatter(t, places):
-            nc.vector.tensor_tensor(zs[t][:].indirect(places[:]), part_a[t][:], part_b[t][:], ADD)
+            nc.vector.tensor_copy(zs[t][:].indirect(places[:]), mix[t][:])
 
         def round_columns(t, h, lo, hi):
             nc.scalar.copy(zs_bf[h][:, lo:hi, t], zs[t][:, h * HALF + lo : h * HALF + hi])
 
-        gather_a(first_plane)
-        gather_b(first_plane)
-        for t, following in zip(PLANE_ORDER, PLANE_ORDER[1:]):
-            gather_a(following)
+        nc.vector.tensor_tensor(terms[first_plane][:, 0:V], y[first_plane][:].indirect(la_sb[:]), share[:, 0:V], MULT)
+        weigh(nc.vector, first_plane, V)
+        add_terms(nc.vector, first_plane)
+        for t in PLANE_ORDER[1:]:
+            weigh(nc.gpsimd, t, 0)
+            add_terms(nc.gpsimd, t)
+        for t in PLANE_ORDER[:-1]:
+            zs[t] = keep.tile([P, S], F32, name=f"zs{t}", align_bytes=64)
             scatter(t, la_sb)
-            gather_b(following)
             scatter(t, lb_sb)
             for h in range(2):
                 round_columns(t, h, 0, HALF)
             if t == first_plane:
                 for m in range(2, ROW_TILES):
                     cast_w2(m)
+        zs[last_plane] = keep.tile([P, S], F32, name=f"zs{last_plane}", align_bytes=64)
         scatter(last_plane, la_sb)
         scatter(last_plane, lb_sb)
 
@@ -185,11 +200,11 @@ def tile_picked_tomein_none_p_kernel(tc, x_words, x_scales, w1, sz, w2, offs, la
                 out=z_code[h][:, lo:hi].bitcast(FP8X4), scales=z_scale[h][:, lo:hi], in_=zs_bf[h][:, lo:hi, :].rearrange("p c j -> p (c j)")
             )
 
-        quantise_w2(0, f"zs{first_plane}")
+        quantise_w2(0, f"terms{last_plane}", f"zs{first_plane}")
         for u in range(3):
             idle = psum.tile([P // 2, S], F32, name=f"idle{u}", tag=f"bank{BANKS - 1 - u}")
             product(idle[:], w2_code[0][:, 0 : P // 2], w2_scale[0][:, 0 : P // 2], x_code[:], x_scale[:])
-        quantise_w2(1, "w2_bf0")
+        quantise_w2(1, "w2_bf0", "w2_scale1")
         for lo, hi in quarters:
             nc.vector.tensor_copy(zs_bf[0][:, lo:hi, last_plane], zs[last_plane][:, lo:hi])
         nc.vector.tensor_copy(zs_bf[1][:, 0:48, last_plane], zs[last_plane][:, HALF : HALF + 48])

@@ -201,9 +201,6 @@ def tile_picked_tomein_none_p_kernel(tc, x_words, x_scales, w1, sz, w2, offs, la
             )
 
         quantise_w2(0, f"terms{last_plane}", f"zs{first_plane}")
-        for u in range(3):
-            idle = psum.tile([P // 2, S], F32, name=f"idle{u}", tag=f"bank{BANKS - 1 - u}")
-            product(idle[:], w2_code[0][:, 0 : P // 2], w2_scale[0][:, 0 : P // 2], x_code[:], x_scale[:])
         quantise_w2(1, "w2_bf0", "w2_scale1")
         for lo, hi in quarters:
             nc.vector.tensor_copy(zs_bf[0][:, lo:hi, last_plane], zs[last_plane][:, lo:hi])

@@ -201,6 +201,9 @@ def tile_picked_tomein_none_p_kernel(tc, x_words, x_scales, w1, sz, w2, offs, la
             )
 
         quantise_w2(0, f"terms{last_plane}", f"zs{first_plane}")
+        for u in range(3):
+            idle = psum.tile([P // 4, S], F32, name=f"idle{u}", tag=f"bank{BANKS - 1 - u}")
+            product(idle[:], w2_code[0][:, 0 : P // 4], w2_scale[0][:, 0 : P // 4], x_code[:], x_scale[:])
         quantise_w2(1, "w2_bf0", "w2_scale1")
         for lo, hi in quarters:
             nc.vector.tensor_copy(zs_bf[0][:, lo:hi, last_plane], zs[last_plane][:, lo:hi])

@@ -26,10 +26,18 @@ ROW_TILES = N // P
 
 PLANE_ORDER = [2, 0, 1, 3]
 
+FIRST_CAST_ON_VECTOR = 80
+LAST_ROUND_ON_VECTOR = 48
+OUT_PIECES_SCALAR_ALONE = 3
+
+WARM_UPS = 3
+WARM_UP_WIDTH = 32
+
 
 def tile_picked_tomein_none_p_kernel(tc, x_words, x_scales, w1, sz, w2, offs, la, lb, out):
     nc = tc.nc
-    first_plane, last_plane = PLANE_ORDER[0], PLANE_ORDER[-1]
+    first_plane, second_plane, third_plane, last_plane = PLANE_ORDER
+    even_planes, odd_planes = PLANE_ORDER[:2], PLANE_ORDER[2:]
     with ExitStack() as ctx:
         keep = ctx.enter_context(tc.tile_pool(name="keep", bufs=1))
         psum = ctx.enter_context(tc.psum_pool(name="psum", bufs=1))
@@ -71,7 +79,6 @@ def tile_picked_tomein_none_p_kernel(tc, x_words, x_scales, w1, sz, w2, offs, la
         x_code = keep.tile([P, S], U32, name="x_code", align_bytes=64)
         nc.vector.tensor_copy(x_code[:], word_table[:].bitcast(U32).indirect(offs_sb[:]))
 
-        even_planes, odd_planes = PLANE_ORDER[:2], PLANE_ORDER[2:]
         w1_bf = {t: keep.tile([P, P, PACK], BF16, name=f"w1_bf{t}", align_bytes=64) for t in even_planes}
         w1_src = [w1_raw[:, 2 * u * H : 2 * (u + 1) * H].rearrange("p (j m t) -> p t m j", j=2, t=PACK) for u in range(2)]
         for t in even_planes:
@@ -80,14 +87,13 @@ def tile_picked_tomein_none_p_kernel(tc, x_words, x_scales, w1, sz, w2, offs, la
         nc.sync.dma_start(share[:, 0:V], sz.rearrange("(p t) v -> p t v", t=PACK)[:, 0, :])
         w2_raw = keep.tile([P, PACK, N], F32, name="w2_raw", tag="big")
         nc.sync.dma_start(w2_raw[:], w2.rearrange("(p j) c -> p j c", j=PACK))
-        nc.scalar.copy(w1_bf[first_plane][:, 80:, 2:4], w1_src[1][:, first_plane, 80:, :])
-        w1_code = {}
-        w1_scale = {}
-        for t in even_planes:
-            width = 80 if t == first_plane else P
+        nc.scalar.copy(w1_bf[first_plane][:, FIRST_CAST_ON_VECTOR:, 2:4], w1_src[1][:, first_plane, FIRST_CAST_ON_VECTOR:, :])
+        w1_codes = keep.tile([P, PACK * P], U32, name="w1_codes", align_bytes=64)
+        w1_scales = keep.tile([P, PACK * P], U8, name="w1_scales", align_bytes=64)
+        w1_code = {t: w1_codes[:, n * P : (n + 1) * P] for n, t in enumerate(PLANE_ORDER)}
+        w1_scale = {t: w1_scales[:, n * P : (n + 1) * P] for n, t in enumerate(PLANE_ORDER)}
+        for t, width in zip(even_planes, (FIRST_CAST_ON_VECTOR, P)):
             nc.vector.tensor_copy(w1_bf[t][:, :width, 2:4], w1_src[1][:, t, :width, :])
-            w1_code[t] = keep.tile([P, P], U32, name=f"w1_code{t}", align_bytes=64)[:]
-            w1_scale[t] = keep.tile([P, P], U8, name=f"w1_scale{t}", align_bytes=64)[:]
             nc.vector.quantize_mx(out=w1_code[t].bitcast(FP8X4), scales=w1_scale[t], in_=w1_bf[t][:].rearrange("p m j -> p (m j)"))
         odd_bf = keep.tile([P, 2 * P * PACK], BF16, name="odd_bf", tag=f"w1_bf{first_plane}", align_bytes=64)
         nc.vector.tensor_copy(
@@ -97,14 +103,10 @@ def tile_picked_tomein_none_p_kernel(tc, x_words, x_scales, w1, sz, w2, offs, la
 
         y = [keep.tile([P, S], F32, name=f"y{t}", align_bytes=64) for t in range(PACK)]
 
-        def make_y(bank, t, lo, hi, on_vector=False):
+        def make_y(bank, t, lo, hi):
             acc = psum.tile([P, hi - lo], F32, name=f"acc_y{bank}", tag=f"bank{bank % BANKS}")
-            for c0 in range(lo, hi, QUARTER):
-                product(acc[:, c0 - lo : c0 - lo + QUARTER], w1_code[t], w1_scale[t], x_code[:, c0 : c0 + QUARTER], x_scale[:, c0 : c0 + QUARTER])
-            if on_vector:
-                nc.vector.tensor_copy(y[t][:, lo:hi], acc[:])
-            else:
-                nc.scalar.copy(y[t][:, lo:hi], acc[:])
+            product(acc[:], w1_code[t], w1_scale[t], x_code[:, lo:hi], x_scale[:, lo:hi])
+            nc.scalar.copy(y[t][:, lo:hi], acc[:])
 
         pair = {t: keep.tile([P, 2 * V], F32, name=f"pair{t}", align_bytes=64) for t in PLANE_ORDER}
         terms = {t: keep.tile([P, 2 * V], F32, name=f"terms{t}", align_bytes=64) for t in PLANE_ORDER}
@@ -113,26 +115,20 @@ def tile_picked_tomein_none_p_kernel(tc, x_words, x_scales, w1, sz, w2, offs, la
             places = (la_sb, lb_sb)[side]
             nc.scalar.activation(pair[t][:, side * V : (side + 1) * V], y[t][:].indirect(places[:]), COPY)
 
-        nc.scalar.activation(share[:, V:], share[:, 0:V], COPY, scale=-1.0, bias=1.0)
-        make_y(0, first_plane, 0, QUARTER)
-        make_y(1, first_plane, QUARTER, HALF)
-        make_y(2, first_plane, HALF, HALF + QUARTER)
-        make_y(3, first_plane, HALF + QUARTER, S)
-        fetch(first_plane, 1)
-        make_y(4, even_planes[1], 0, HALF)
-        make_y(5, even_planes[1], HALF, S)
-        fetch(even_planes[1], 0)
-        fetch(even_planes[1], 1)
-        odd_code = keep.tile([P, 2 * P], U32, name="odd_code", tag=f"w1_code{first_plane}", align_bytes=64)
-        odd_scale = keep.tile([P, 2 * P], U8, name="odd_scale", align_bytes=64)
-        nc.vector.quantize_mx(out=odd_code[:].bitcast(FP8X4), scales=odd_scale[:], in_=odd_bf[:])
-        for e, t in enumerate(odd_planes):
-            w1_code[t] = odd_code[:, e * P : (e + 1) * P]
-            w1_scale[t] = odd_scale[:, e * P : (e + 1) * P]
-            make_y(6 + 2 * e, t, 0, HALF)
-            make_y(7 + 2 * e, t, HALF, S)
+        def make_and_fetch(bank, t):
+            make_y(bank, t, 0, HALF)
+            make_y(bank + 1, t, HALF, S)
             fetch(t, 0)
             fetch(t, 1)
+
+        nc.scalar.activation(share[:, V:], share[:, 0:V], COPY, scale=-1.0, bias=1.0)
+        for q in range(4):
+            make_y(q, first_plane, q * QUARTER, (q + 1) * QUARTER)
+        fetch(first_plane, 1)
+        make_and_fetch(4, second_plane)
+        nc.vector.quantize_mx(out=w1_codes[:, 2 * P :].bitcast(FP8X4), scales=w1_scales[:, 2 * P :], in_=odd_bf[:])
+        make_and_fetch(6, third_plane)
+        make_and_fetch(8, last_plane)
 
         w2_bf = [keep.tile([P, 2 * P, PACK], BF16, name=f"w2_bf{u}", align_bytes=64) for u in range(2)]
         w2_code = {}
@@ -144,9 +140,9 @@ def tile_picked_tomein_none_p_kernel(tc, x_words, x_scales, w1, sz, w2, offs, la
                 w2_raw[:, :, m * P : (m + 1) * P].rearrange("p j (c i) -> p c j i", i=4),
             )
 
-        def quantise_w2(u, after, scale_after):
-            code = keep.tile([P, 2 * P], U32, name=f"w2_code{u}", tag=after, align_bytes=64)
-            scale = keep.tile([P, 2 * P], U8, name=f"w2_scale{u}", tag=scale_after, align_bytes=64)
+        def quantise_w2(u, code_tag, scale_tag):
+            code = keep.tile([P, 2 * P], U32, name=f"w2_code{u}", tag=code_tag, align_bytes=64)
+            scale = keep.tile([P, 2 * P], U8, name=f"w2_scale{u}", tag=scale_tag, align_bytes=64)
             nc.vector.quantize_mx(out=code[:].bitcast(FP8X4), scales=scale[:], in_=w2_bf[u][:].rearrange("p c j -> p (c j)"))
             for e in range(2):
                 w2_code[2 * u + e] = code[:, e * P : (e + 1) * P]
@@ -155,9 +151,8 @@ def tile_picked_tomein_none_p_kernel(tc, x_words, x_scales, w1, sz, w2, offs, la
         cast_w2(0)
         cast_w2(1)
 
-        zs_bf = [keep.tile([P, HALF, PACK], BF16, name=f"zs_bf{h}", tag=f"y{PLANE_ORDER[-1 - h]}", align_bytes=64) for h in range(2)]
+        zs_bf = [keep.tile([P, HALF, PACK], BF16, name=f"zs_bf{h}", tag=f"y{t}", align_bytes=64) for h, t in enumerate((last_plane, third_plane))]
         zs = {}
-
         mix = {t: keep.tile([P, V], F32, name=f"mix{t}", align_bytes=64) for t in PLANE_ORDER}
 
         def weigh(engine, t, lo):
@@ -166,8 +161,10 @@ def tile_picked_tomein_none_p_kernel(tc, x_words, x_scales, w1, sz, w2, offs, la
         def add_terms(engine, t):
             engine.tensor_tensor(mix[t][:], terms[t][:, 0:V], terms[t][:, V:], ADD)
 
-        def scatter(t, places):
-            nc.vector.tensor_copy(zs[t][:].indirect(places[:]), mix[t][:])
+        def scatter_plane(t):
+            zs[t] = keep.tile([P, S], F32, name=f"zs{t}", align_bytes=64)
+            for places in (la_sb, lb_sb):
+                nc.vector.tensor_copy(zs[t][:].indirect(places[:]), mix[t][:])
 
         def round_columns(t, h, lo, hi):
             nc.scalar.copy(zs_bf[h][:, lo:hi, t], zs[t][:, h * HALF + lo : h * HALF + hi])
@@ -179,57 +176,47 @@ def tile_picked_tomein_none_p_kernel(tc, x_words, x_scales, w1, sz, w2, offs, la
             weigh(nc.gpsimd, t, 0)
             add_terms(nc.gpsimd, t)
         for t in PLANE_ORDER[:-1]:
-            zs[t] = keep.tile([P, S], F32, name=f"zs{t}", align_bytes=64)
-            scatter(t, la_sb)
-            scatter(t, lb_sb)
+            scatter_plane(t)
             for h in range(2):
                 round_columns(t, h, 0, HALF)
             if t == first_plane:
-                for m in range(2, ROW_TILES):
-                    cast_w2(m)
-        zs[last_plane] = keep.tile([P, S], F32, name=f"zs{last_plane}", align_bytes=64)
-        scatter(last_plane, la_sb)
-        scatter(last_plane, lb_sb)
+                cast_w2(2)
+                cast_w2(3)
+        scatter_plane(last_plane)
 
         z_code = [keep.tile([P, HALF], U32, name=f"z_code{h}", align_bytes=64) for h in range(2)]
         z_scale = [keep.tile([P, HALF], U8, name=f"z_scale{h}", align_bytes=64) for h in range(2)]
         quarters = [(0, QUARTER), (QUARTER, HALF)]
 
-        def quantise_zs(h, lo, hi):
-            nc.vector.quantize_mx(
-                out=z_code[h][:, lo:hi].bitcast(FP8X4), scales=z_scale[h][:, lo:hi], in_=zs_bf[h][:, lo:hi, :].rearrange("p c j -> p (c j)")
-            )
-
         quantise_w2(0, f"terms{last_plane}", f"zs{first_plane}")
-        for u in range(3):
-            idle = psum.tile([P // 4, S], F32, name=f"idle{u}", tag=f"bank{BANKS - 1 - u}")
-            product(idle[:], w2_code[0][:, 0 : P // 4], w2_scale[0][:, 0 : P // 4], x_code[:], x_scale[:])
+        for u in range(WARM_UPS):
+            idle = psum.tile([WARM_UP_WIDTH, S], F32, name=f"idle{u}", tag=f"bank{BANKS - 1 - u}")
+            product(idle[:], w2_code[0][:, 0:WARM_UP_WIDTH], w2_scale[0][:, 0:WARM_UP_WIDTH], w1_codes[:], w1_scales[:])
         quantise_w2(1, "w2_bf0", "w2_scale1")
+
         for lo, hi in quarters:
             nc.vector.tensor_copy(zs_bf[0][:, lo:hi, last_plane], zs[last_plane][:, lo:hi])
-        nc.vector.tensor_copy(zs_bf[1][:, 0:48, last_plane], zs[last_plane][:, HALF : HALF + 48])
-        round_columns(last_plane, 1, 48, HALF)
-        for lo, hi in quarters:
-            quantise_zs(0, lo, hi)
-        quantise_zs(1, *quarters[0])
-        quantise_zs(1, *quarters[1])
+        nc.vector.tensor_copy(zs_bf[1][:, 0:LAST_ROUND_ON_VECTOR, last_plane], zs[last_plane][:, HALF : HALF + LAST_ROUND_ON_VECTOR])
+        round_columns(last_plane, 1, LAST_ROUND_ON_VECTOR, HALF)
+        for h in range(2):
+            for lo, hi in quarters:
+                nc.vector.quantize_mx(
+                    out=z_code[h][:, lo:hi].bitcast(FP8X4), scales=z_scale[h][:, lo:hi], in_=zs_bf[h][:, lo:hi, :].rearrange("p c j -> p (c j)")
+                )
 
         res = [keep.tile([P, S], F32, name=f"res{m}") for m in range(ROW_TILES)]
-        scalar_alone, stored_by_halves = 3, 4
-        out_pieces = [(0, 0, lo, hi) for lo, hi in quarters] + [(m, 0, 0, HALF) for m in range(1, ROW_TILES - 1)]
-        out_pieces = out_pieces + [(m, 1, 0, HALF) for m in range(ROW_TILES - 1)] + [(ROW_TILES - 1, h, 0, HALF) for h in range(2)]
+        last_tile = ROW_TILES - 1
+        out_pieces = [(0, 0, lo, hi) for lo, hi in quarters] + [(m, 0, 0, HALF) for m in range(1, last_tile)]
+        out_pieces = out_pieces + [(m, 1, 0, HALF) for m in range(last_tile)] + [(last_tile, h, 0, HALF) for h in range(2)]
         for n, (m, h, lo, hi) in enumerate(out_pieces):
             acc = psum.tile([P, hi - lo], F32, name=f"acc_out{n}", tag=f"bank{n % BANKS}")
-            for c0, c1 in quarters if m < ROW_TILES - 1 and hi - lo == HALF else [(lo, hi)]:
+            for c0, c1 in quarters if m < last_tile and hi - lo == HALF else [(lo, hi)]:
                 product(acc[:, c0 - lo : c1 - lo], w2_code[m], w2_scale[m], z_code[h][:, c0:c1], z_scale[h][:, c0:c1])
             piece = res[m][:, h * HALF + lo : h * HALF + hi]
-            if n >= scalar_alone and (n - scalar_alone) % 2 == 0:
+            if n >= OUT_PIECES_SCALAR_ALONE and (n - OUT_PIECES_SCALAR_ALONE) % 2 == 0:
                 nc.vector.tensor_copy(piece, acc[:])
             else:
                 nc.scalar.copy(piece, acc[:])
-            rows = slice(m * P, (m + 1) * P)
-            if m < stored_by_halves and hi == HALF:
+            if hi == HALF:
                 cols = slice(h * HALF, (h + 1) * HALF)
-                nc.sync.dma_start(out[rows, cols], res[m][:, cols])
-            elif h == 1:
-                nc.sync.dma_start(out[rows, :], res[m][:])
+                nc.sync.dma_start(out[m * P : (m + 1) * P, cols], res[m][:, cols])

@@ -22,6 +22,7 @@ PACK = 4
 BANKS = 8
 HALF = S // 2
 QUARTER = S // 4
+PART = V // 2
 ROW_TILES = N // P
 
 PLANE_ORDER = [2, 0, 1, 3]
@@ -108,27 +109,41 @@ def tile_picked_tomein_none_p_kernel(tc, x_words, x_scales, w1, sz, w2, offs, la
             product(acc[:], w1_code[t], w1_scale[t], x_code[:, lo:hi], x_scale[:, lo:hi])
             nc.scalar.copy(y[t][:, lo:hi], acc[:])
 
-        pair = {t: keep.tile([P, 2 * V], F32, name=f"pair{t}", align_bytes=64) for t in PLANE_ORDER}
-        terms = {t: keep.tile([P, 2 * V], F32, name=f"terms{t}", align_bytes=64) for t in PLANE_ORDER}
+        alone = (first_plane, last_plane)
+        twins = (second_plane, third_plane)
+        pair = {t: keep.tile([P, 2 * V], F32, name=f"pair{t}", align_bytes=64) for t in (last_plane,)}
+        terms = {t: keep.tile([P, 2 * V], F32, name=f"terms{t}", align_bytes=64) for t in alone}
+        twin_pair = [keep.tile([P, 2, 2, PART], F32, name=f"twin_pair{h}", align_bytes=64) for h in range(2)]
+        twin_mix = [keep.tile([P, 2, PART], F32, name=f"twin_mix{h}", align_bytes=64) for h in range(2)]
+
+        def list_half(side, h):
+            return (la_sb, lb_sb)[side][:, h * PART // 16 : (h + 1) * PART // 16]
+
+        def fetch_half(n, h):
+            for side in range(2):
+                nc.scalar.activation(twin_pair[h][:, n, side, :], y[twins[n]][:].indirect(list_half(side, h)), COPY)
 
         def fetch(t, side):
             places = (la_sb, lb_sb)[side]
             nc.scalar.activation(pair[t][:, side * V : (side + 1) * V], y[t][:].indirect(places[:]), COPY)
 
-        def make_and_fetch(bank, t):
+        def make_halves(bank, t):
             make_y(bank, t, 0, HALF)
             make_y(bank + 1, t, HALF, S)
-            fetch(t, 0)
-            fetch(t, 1)
 
         nc.scalar.activation(share[:, V:], share[:, 0:V], COPY, scale=-1.0, bias=1.0)
         for q in range(4):
             make_y(q, first_plane, q * QUARTER, (q + 1) * QUARTER)
-        fetch(first_plane, 1)
-        make_and_fetch(4, second_plane)
+        make_halves(4, second_plane)
+        fetch_half(0, 0)
         nc.vector.quantize_mx(out=w1_codes[:, 2 * P :].bitcast(FP8X4), scales=w1_scales[:, 2 * P :], in_=odd_bf[:])
-        make_and_fetch(6, third_plane)
-        make_and_fetch(8, last_plane)
+        make_halves(6, third_plane)
+        fetch_half(1, 0)
+        fetch_half(0, 1)
+        fetch_half(1, 1)
+        make_halves(8, last_plane)
+        fetch(last_plane, 0)
+        fetch(last_plane, 1)
 
         w2_bf = [keep.tile([P, 2 * P, PACK], BF16, name=f"w2_bf{u}", align_bytes=64) for u in range(2)]
         w2_code = {}
@@ -153,7 +168,7 @@ def tile_picked_tomein_none_p_kernel(tc, x_words, x_scales, w1, sz, w2, offs, la
 
         zs_bf = [keep.tile([P, HALF, PACK], BF16, name=f"zs_bf{h}", tag=f"y{t}", align_bytes=64) for h, t in enumerate((last_plane, third_plane))]
         zs = {}
-        mix = {t: keep.tile([P, V], F32, name=f"mix{t}", align_bytes=64) for t in PLANE_ORDER}
+        mix = {t: keep.tile([P, V], F32, name=f"mix{t}", align_bytes=64) for t in alone}
 
         def weigh(engine, t, lo):
             engine.tensor_tensor(terms[t][:, lo:], pair[t][:, lo:], share[:, lo:], MULT)
@@ -169,19 +184,32 @@ def tile_picked_tomein_none_p_kernel(tc, x_words, x_scales, w1, sz, w2, offs, la
         def round_columns(t, h, lo, hi):
             nc.scalar.copy(zs_bf[h][:, lo:hi, t], zs[t][:, h * HALF + lo : h * HALF + hi])
 
-        nc.vector.tensor_tensor(terms[first_plane][:, 0:V], y[first_plane][:].indirect(la_sb[:]), share[:, 0:V], MULT)
-        weigh(nc.vector, first_plane, V)
+        for side, places in enumerate((la_sb, lb_sb)):
+            cols = slice(side * V, (side + 1) * V)
+            nc.vector.tensor_tensor(terms[first_plane][:, cols], y[first_plane][:].indirect(places[:]), share[:, cols], MULT)
         add_terms(nc.vector, first_plane)
-        for t in PLANE_ORDER[1:]:
-            weigh(nc.gpsimd, t, 0)
-            add_terms(nc.gpsimd, t)
-        for t in PLANE_ORDER[:-1]:
-            scatter_plane(t)
+        share_sides = share[:].rearrange("p (s v) -> p s v", s=2)
+        for h in range(2):
+            twin_terms = keep.tile([P, 2, 2, PART], F32, name="twin_terms", tag=f"terms{first_plane}", align_bytes=64)
+            for n in range(2):
+                nc.gpsimd.tensor_tensor(twin_terms[:, n], twin_pair[h][:, n], share_sides[:, :, h * PART : (h + 1) * PART], MULT)
+            nc.gpsimd.tensor_tensor(twin_mix[h][:], twin_terms[:, :, 0, :], twin_terms[:, :, 1, :], ADD)
+        weigh(nc.gpsimd, last_plane, 0)
+        add_terms(nc.gpsimd, last_plane)
+        scatter_plane(first_plane)
+        for h in range(2):
+            round_columns(first_plane, h, 0, HALF)
+        cast_w2(2)
+        cast_w2(3)
+        for t in twins:
+            zs[t] = keep.tile([P, S], F32, name=f"zs{t}", align_bytes=64)
+        for h in range(2):
+            for side in range(2):
+                for n, t in enumerate(twins):
+                    nc.vector.tensor_copy(zs[t][:].indirect(list_half(side, h)), twin_mix[h][:, n, :])
+        for t in twins:
             for h in range(2):
                 round_columns(t, h, 0, HALF)
-            if t == first_plane:
-                cast_w2(2)
-                cast_w2(3)
         scatter_plane(last_plane)
 
         z_code = [keep.tile([P, HALF], U32, name=f"z_code{h}", align_bytes=64) for h in range(2)]

@@ -22,7 +22,6 @@ PACK = 4
 BANKS = 8
 HALF = S // 2
 QUARTER = S // 4
-PART = V // 2
 ROW_TILES = N // P
 
 PLANE_ORDER = [2, 0, 1, 3]
@@ -109,41 +108,29 @@ def tile_picked_tomein_none_p_kernel(tc, x_words, x_scales, w1, sz, w2, offs, la
             product(acc[:], w1_code[t], w1_scale[t], x_code[:, lo:hi], x_scale[:, lo:hi])
             nc.scalar.copy(y[t][:, lo:hi], acc[:])
 
-        alone = (first_plane, last_plane)
-        twins = (second_plane, third_plane)
-        pair = {t: keep.tile([P, 2 * V], F32, name=f"pair{t}", align_bytes=64) for t in (last_plane,)}
-        terms = {t: keep.tile([P, 2 * V], F32, name=f"terms{t}", align_bytes=64) for t in alone}
-        twin_pair = [keep.tile([P, 2, 2, PART], F32, name=f"twin_pair{h}", align_bytes=64) for h in range(2)]
-        twin_mix = [keep.tile([P, 2, PART], F32, name=f"twin_mix{h}", align_bytes=64) for h in range(2)]
+        pair = {t: keep.tile([P, 2 * V], F32, name=f"pair{t}", align_bytes=64) for t in PLANE_ORDER[1:]}
+        terms = {}
 
-        def list_half(side, h):
-            return (la_sb, lb_sb)[side][:, h * PART // 16 : (h + 1) * PART // 16]
-
-        def fetch_half(n, h):
-            for side in range(2):
-                nc.scalar.activation(twin_pair[h][:, n, side, :], y[twins[n]][:].indirect(list_half(side, h)), COPY)
+        def new_terms(t):
+            terms[t] = keep.tile([P, 2 * V], F32, name=f"terms{t}", tag="terms", align_bytes=64)
 
         def fetch(t, side):
             places = (la_sb, lb_sb)[side]
             nc.scalar.activation(pair[t][:, side * V : (side + 1) * V], y[t][:].indirect(places[:]), COPY)
 
-        def make_halves(bank, t):
+        def make_and_fetch(bank, t):
             make_y(bank, t, 0, HALF)
             make_y(bank + 1, t, HALF, S)
+            fetch(t, 0)
+            fetch(t, 1)
 
         nc.scalar.activation(share[:, V:], share[:, 0:V], COPY, scale=-1.0, bias=1.0)
         for q in range(4):
             make_y(q, first_plane, q * QUARTER, (q + 1) * QUARTER)
-        make_halves(4, second_plane)
-        fetch_half(0, 0)
+        make_and_fetch(4, second_plane)
         nc.vector.quantize_mx(out=w1_codes[:, 2 * P :].bitcast(FP8X4), scales=w1_scales[:, 2 * P :], in_=odd_bf[:])
-        make_halves(6, third_plane)
-        fetch_half(1, 0)
-        fetch_half(0, 1)
-        fetch_half(1, 1)
-        make_halves(8, last_plane)
-        fetch(last_plane, 0)
-        fetch(last_plane, 1)
+        make_and_fetch(6, third_plane)
+        make_and_fetch(8, last_plane)
 
         w2_bf = [keep.tile([P, 2 * P, PACK], BF16, name=f"w2_bf{u}", align_bytes=64) for u in range(2)]
         w2_code = {}
@@ -168,55 +155,66 @@ def tile_picked_tomein_none_p_kernel(tc, x_words, x_scales, w1, sz, w2, offs, la
 
         zs_bf = [keep.tile([P, HALF, PACK], BF16, name=f"zs_bf{h}", tag=f"y{t}", align_bytes=64) for h, t in enumerate((last_plane, third_plane))]
         zs = {}
-        mix = {t: keep.tile([P, V], F32, name=f"mix{t}", align_bytes=64) for t in alone}
+        mixes = keep.tile([P, 2 * V], F32, name="mixes", align_bytes=64)
+        first_mix = keep.tile([P, V], F32, name="first_mix", align_bytes=64)
+        mix = {first_plane: first_mix[:], second_plane: mixes[:, 0:V], third_plane: mixes[:, V:]}
 
-        def weigh(engine, t, lo):
-            engine.tensor_tensor(terms[t][:, lo:], pair[t][:, lo:], share[:, lo:], MULT)
+        def weigh(t, lo, hi):
+            nc.gpsimd.tensor_tensor(terms[t][:, lo:hi], pair[t][:, lo:hi], share[:, lo:hi], MULT)
 
         def add_terms(engine, t):
-            engine.tensor_tensor(mix[t][:], terms[t][:, 0:V], terms[t][:, V:], ADD)
+            engine.tensor_tensor(mix[t], terms[t][:, 0:V], terms[t][:, V:], ADD)
 
         def scatter_plane(t):
             zs[t] = keep.tile([P, S], F32, name=f"zs{t}", align_bytes=64)
             for places in (la_sb, lb_sb):
-                nc.vector.tensor_copy(zs[t][:].indirect(places[:]), mix[t][:])
+                nc.vector.tensor_copy(zs[t][:].indirect(places[:]), mix[t])
 
         def round_columns(t, h, lo, hi):
             nc.scalar.copy(zs_bf[h][:, lo:hi, t], zs[t][:, h * HALF + lo : h * HALF + hi])
 
+        def round_plane(t):
+            for h in range(2):
+                round_columns(t, h, 0, HALF)
+
+        new_terms(first_plane)
         for side, places in enumerate((la_sb, lb_sb)):
             cols = slice(side * V, (side + 1) * V)
             nc.vector.tensor_tensor(terms[first_plane][:, cols], y[first_plane][:].indirect(places[:]), share[:, cols], MULT)
         add_terms(nc.vector, first_plane)
-        share_sides = share[:].rearrange("p (s v) -> p s v", s=2)
-        for h in range(2):
-            twin_terms = keep.tile([P, 2, 2, PART], F32, name="twin_terms", tag=f"terms{first_plane}", align_bytes=64)
-            for n in range(2):
-                nc.gpsimd.tensor_tensor(twin_terms[:, n], twin_pair[h][:, n], share_sides[:, :, h * PART : (h + 1) * PART], MULT)
-            nc.gpsimd.tensor_tensor(twin_mix[h][:], twin_terms[:, :, 0, :], twin_terms[:, :, 1, :], ADD)
-        weigh(nc.gpsimd, last_plane, 0)
-        add_terms(nc.gpsimd, last_plane)
+        new_terms(second_plane)
+        weigh(second_plane, 0, V)
+        weigh(second_plane, V, 2 * V)
+        add_terms(nc.gpsimd, second_plane)
+        new_terms(third_plane)
+        weigh(third_plane, 0, 2 * V)
+        add_terms(nc.gpsimd, third_plane)
+        new_terms(last_plane)
+        weigh(last_plane, 0, 2 * V)
         scatter_plane(first_plane)
-        for h in range(2):
-            round_columns(first_plane, h, 0, HALF)
+        twins = (second_plane, third_plane)
+        twin_mix = keep.tile([P, 2 * V], F32, name="twin_mix", align_bytes=64)
+        nc.scalar.copy(twin_mix[:], mixes[:])
+        round_plane(first_plane)
         cast_w2(2)
         cast_w2(3)
         for t in twins:
             zs[t] = keep.tile([P, S], F32, name=f"zs{t}", align_bytes=64)
-        for h in range(2):
-            for side in range(2):
-                for n, t in enumerate(twins):
-                    nc.vector.tensor_copy(zs[t][:].indirect(list_half(side, h)), twin_mix[h][:, n, :])
+            nc.vector.tensor_copy(zs[t][:].indirect(la_sb[:]), mix[t])
+        last_mix = keep.tile([P, V], F32, name="last_mix", tag="mixes", align_bytes=64)
+        mix[last_plane] = last_mix[:]
+        add_terms(nc.gpsimd, last_plane)
+        for n, t in enumerate(twins):
+            nc.vector.tensor_copy(zs[t][:].indirect(lb_sb[:]), twin_mix[:, n * V : (n + 1) * V])
         for t in twins:
-            for h in range(2):
-                round_columns(t, h, 0, HALF)
+            round_plane(t)
         scatter_plane(last_plane)
 
         z_code = [keep.tile([P, HALF], U32, name=f"z_code{h}", align_bytes=64) for h in range(2)]
         z_scale = [keep.tile([P, HALF], U8, name=f"z_scale{h}", align_bytes=64) for h in range(2)]
         quarters = [(0, QUARTER), (QUARTER, HALF)]
 
-        quantise_w2(0, f"terms{last_plane}", f"zs{first_plane}")
+        quantise_w2(0, "terms", f"zs{first_plane}")
         for u in range(WARM_UPS):
             idle = psum.tile([WARM_UP_WIDTH, S], F32, name=f"idle{u}", tag=f"bank{BANKS - 1 - u}")
             product(idle[:], w2_code[0][:, 0:WARM_UP_WIDTH], w2_scale[0][:, 0:WARM_UP_WIDTH], w1_codes[:], w1_scales[:])

@@ -79,6 +79,10 @@ def tile_picked_tomein_none_p_kernel(tc, x_words, x_scales, w1, sz, w2, offs, la
         x_code = keep.tile([P, S], U32, name="x_code", align_bytes=64)
         nc.vector.tensor_copy(x_code[:], word_table[:].bitcast(U32).indirect(offs_sb[:]))
 
+        windows = [keep.tile([P, S], F32, name=f"window{side}", align_bytes=64) for side in range(2)]
+        for window in windows:
+            nc.vector.memset(window[:], 0.0)
+
         w1_bf = {t: keep.tile([P, P, PACK], BF16, name=f"w1_bf{t}", align_bytes=64) for t in even_planes}
         w1_src = [w1_raw[:, 2 * u * H : 2 * (u + 1) * H].rearrange("p (j m t) -> p t m j", j=2, t=PACK) for u in range(2)]
         for t in even_planes:
@@ -127,7 +131,9 @@ def tile_picked_tomein_none_p_kernel(tc, x_words, x_scales, w1, sz, w2, offs, la
         nc.scalar.activation(share[:, V:], share[:, 0:V], COPY, scale=-1.0, bias=1.0)
         for q in range(4):
             make_y(q, first_plane, q * QUARTER, (q + 1) * QUARTER)
-        make_and_fetch(4, second_plane)
+        make_y(4, second_plane, 0, HALF)
+        make_y(5, second_plane, HALF, S)
+        fetch(second_plane, 1)
         nc.vector.quantize_mx(out=w1_codes[:, 2 * P :].bitcast(FP8X4), scales=w1_scales[:, 2 * P :], in_=odd_bf[:])
         make_and_fetch(6, third_plane)
         make_and_fetch(8, last_plane)
@@ -153,7 +159,6 @@ def tile_picked_tomein_none_p_kernel(tc, x_words, x_scales, w1, sz, w2, offs, la
         cast_w2(0)
         cast_w2(1)
 
-        zs_bf = [keep.tile([P, HALF, PACK], BF16, name=f"zs_bf{h}", tag=f"y{t}", align_bytes=64) for h, t in enumerate((last_plane, third_plane))]
         zs = {}
         mixes = keep.tile([P, 2 * V], F32, name="mixes", align_bytes=64)
         first_mix = keep.tile([P, V], F32, name="first_mix", align_bytes=64)
@@ -182,16 +187,24 @@ def tile_picked_tomein_none_p_kernel(tc, x_words, x_scales, w1, sz, w2, offs, la
             cols = slice(side * V, (side + 1) * V)
             nc.vector.tensor_tensor(terms[first_plane][:, cols], y[first_plane][:].indirect(places[:]), share[:, cols], MULT)
         add_terms(nc.vector, first_plane)
-        new_terms(second_plane)
-        weigh(second_plane, 0, V)
+        early_term = keep.tile([P, V], F32, name="early_term", align_bytes=64)
+        for lo in (0, V // 2):
+            cols = slice(lo, lo + V // 2)
+            nc.vector.tensor_tensor(early_term[:, cols], y[second_plane][:].indirect(la_sb[:, lo // 16 : (lo + V // 2) // 16]), share[:, cols], MULT)
+        terms[second_plane] = keep.tile([P, 2 * V], F32, name="second_terms", tag=f"y{second_plane}", align_bytes=64)
         weigh(second_plane, V, 2 * V)
-        add_terms(nc.gpsimd, second_plane)
-        new_terms(third_plane)
-        weigh(third_plane, 0, 2 * V)
-        add_terms(nc.gpsimd, third_plane)
-        new_terms(last_plane)
+        third_terms = [keep.tile([P, V], F32, name=f"third_term{side}", align_bytes=64) for side in range(2)]
+        nc.gpsimd.tensor_tensor(third_terms[0][:], pair[third_plane][:, 0:V], share[:, 0:V], MULT)
+        nc.gpsimd.tensor_tensor(mix[second_plane], early_term[:], terms[second_plane][:, V:], ADD)
+        nc.gpsimd.tensor_tensor(third_terms[1][:], pair[third_plane][:, V:], share[:, V:], MULT)
+        nc.gpsimd.tensor_tensor(mix[third_plane], third_terms[0][:], third_terms[1][:], ADD)
+        for window, places in zip(windows, (la_sb, lb_sb)):
+            nc.vector.tensor_copy(window[:].indirect(places[:]), mix[first_plane])
+        zs[first_plane] = keep.tile([P, S], F32, name="first_sum", tag="third_term0", align_bytes=64)
+        nc.gpsimd.tensor_tensor(zs[first_plane][:], windows[0][:], windows[1][:], ADD)
+        terms[last_plane] = keep.tile([P, 2 * V], F32, name="last_terms", tag="third_term1", align_bytes=64)
         weigh(last_plane, 0, 2 * V)
-        scatter_plane(first_plane)
+        zs_bf = [keep.tile([P, HALF, PACK], BF16, name=f"zs_bf{h}", tag=f"window{h}", align_bytes=64) for h in range(2)]
         twins = (second_plane, third_plane)
         twin_mix = keep.tile([P, 2 * V], F32, name="twin_mix", align_bytes=64)
         nc.scalar.copy(twin_mix[:], mixes[:])
@@ -214,7 +227,7 @@ def tile_picked_tomein_none_p_kernel(tc, x_words, x_scales, w1, sz, w2, offs, la
         z_scale = [keep.tile([P, HALF], U8, name=f"z_scale{h}", align_bytes=64) for h in range(2)]
         quarters = [(0, QUARTER), (QUARTER, HALF)]
 
-        quantise_w2(0, "terms", f"zs{first_plane}")
+        quantise_w2(0, "third_term1", "third_term0")
         for u in range(WARM_UPS):
             idle = psum.tile([WARM_UP_WIDTH, S], F32, name=f"idle{u}", tag=f"bank{BANKS - 1 - u}")
             product(idle[:], w2_code[0][:, 0:WARM_UP_WIDTH], w2_scale[0][:, 0:WARM_UP_WIDTH], w1_codes[:], w1_scales[:])

from contextlib import ExitStack

import concourse.mybir as mybir

K, T, S, V, N, H = 512, 2048, 512, 256, 512, 512
FLOPS = 2 * K * H * S + 2 * H * N * S
BYTES = K * T + K * T // 32 + 4 * K * H + 4 * 8 * V + 4 * H * N + 2 * 128 * (S + 2 * V) // 16 + 4 * N * S

F32 = mybir.dt.float32
BF16 = mybir.dt.bfloat16
I32 = mybir.dt.int32
U32 = mybir.dt.uint32
U16 = mybir.dt.uint16
U8 = mybir.dt.uint8
FP8X4 = mybir.dt.float8_e4m3fn_x4
MULT = mybir.AluOpType.mult
ADD = mybir.AluOpType.add
COPY = mybir.ActivationFunctionType.Copy

P = 128
PACK = 4
BANKS = 8
HALF = S // 2
QUARTER = S // 4
ROW_TILES = N // P

PLANE_ORDER = [2, 0, 1, 3]

FIRST_CAST_ON_VECTOR = 80
LAST_ROUND_ON_VECTOR = 48
OUT_PIECES_SCALAR_ALONE = 3

WARM_UPS = 3
WARM_UP_WIDTH = 32


def tile_picked_tomein_none_p_kernel(tc, x_words, x_scales, w1, sz, w2, offs, la, lb, out):
    nc = tc.nc
    first_plane, second_plane, third_plane, last_plane = PLANE_ORDER
    even_planes, odd_planes = PLANE_ORDER[:2], PLANE_ORDER[2:]
    with ExitStack() as ctx:
        keep = ctx.enter_context(tc.tile_pool(name="keep", bufs=1))
        psum = ctx.enter_context(tc.psum_pool(name="psum", bufs=1))

        def product(acc, still_code, still_scale, moving_code, moving_scale):
            nc.tensor.matmul_mx(
                out=acc,
                lhsT=still_code.bitcast(FP8X4),
                lhsT_scale=still_scale,
                rhs=moving_code.bitcast(FP8X4),
                rhs_scale=moving_scale,
                start=True,
                stop=True,
            )

        offs_sb = keep.tile([P, S // 16], U16, name="offs_sb")
        la_sb = keep.tile([P, V // 16], U16, name="la_sb")
        lb_sb = keep.tile([P, V // 16], U16, name="lb_sb")
        word_table = keep.tile([P, T], I32, name="word_table", tag="big")
        scale_table = keep.tile([P, T], U8, name="scale_table")
        w1_raw = keep.tile([P, PACK * H], F32, name="w1_raw")

        nc.vector.memset(scale_table[:].bitcast(I32), 0)
        w1_rows = w1.rearrange("(p j) c -> p (j c)", j=PACK)
        nc.sync.dma_start(w1_raw[:, 0 : 2 * H], w1_rows[:, 0 : 2 * H])
        nc.sync.dma_start(offs_sb[:], offs)
        nc.sync.dma_start(scale_table[0:P:8, :].bitcast(I32), x_scales[0].bitcast(I32))
        nc.sync.dma_start(word_table[:], x_words[0].rearrange("p n t -> p (n t)").bitcast(I32))
        nc.sync.dma_start(w1_raw[:, 2 * H : 4 * H], w1_rows[:, 2 * H : 4 * H])
        nc.sync.dma_start(la_sb[:], la)
        nc.sync.dma_start(lb_sb[:], lb)

        picked = keep.tile([P, S], U8, name="picked", align_bytes=64)
        nc.vector.tensor_copy(picked[:], scale_table[:].indirect(offs_sb[:]))
        x_scale = keep.tile([P, S], U8, name="x_scale", align_bytes=64)
        nc.vector.memset(x_scale[:].bitcast(I32), 0)
        for r in range(4):
            nc.sync.dma_start(x_scale[r:P:32, :].bitcast(I32), picked[8 * r : P : 32, :].bitcast(I32))
        x_code = keep.tile([P, S], U32, name="x_code", align_bytes=64)
        nc.vector.tensor_copy(x_code[:], word_table[:].bitcast(U32).indirect(offs_sb[:]))

        windows = [keep.tile([P, S], F32, name=f"window{side}", align_bytes=64) for side in range(2)]
        for window in windows:
            nc.vector.memset(window[:], 0.0)

        w1_bf = {t: keep.tile([P, P, PACK], BF16, name=f"w1_bf{t}", align_bytes=64) for t in even_planes}
        w1_src = [w1_raw[:, 2 * u * H : 2 * (u + 1) * H].rearrange("p (j m t) -> p t m j", j=2, t=PACK) for u in range(2)]
        for t in even_planes:
            nc.scalar.copy(w1_bf[t][:, :, 0:2], w1_src[0][:, t])
        share = keep.tile([P, 2 * V], F32, name="share", tag="scale_table")
        nc.sync.dma_start(share[:, 0:V], sz.rearrange("(p t) v -> p t v", t=PACK)[:, 0, :])
        w2_raw = keep.tile([P, PACK, N], F32, name="w2_raw", tag="big")
        nc.sync.dma_start(w2_raw[:], w2.rearrange("(p j) c -> p j c", j=PACK))
        nc.scalar.copy(w1_bf[first_plane][:, FIRST_CAST_ON_VECTOR:, 2:4], w1_src[1][:, first_plane, FIRST_CAST_ON_VECTOR:, :])
        w1_codes = keep.tile([P, PACK * P], U32, name="w1_codes", align_bytes=64)
        w1_scales = keep.tile([P, PACK * P], U8, name="w1_scales", align_bytes=64)
        w1_code = {t: w1_codes[:, n * P : (n + 1) * P] for n, t in enumerate(PLANE_ORDER)}
        w1_scale = {t: w1_scales[:, n * P : (n + 1) * P] for n, t in enumerate(PLANE_ORDER)}
        for t, width in zip(even_planes, (FIRST_CAST_ON_VECTOR, P)):
            nc.vector.tensor_copy(w1_bf[t][:, :width, 2:4], w1_src[1][:, t, :width, :])
            nc.vector.quantize_mx(out=w1_code[t].bitcast(FP8X4), scales=w1_scale[t], in_=w1_bf[t][:].rearrange("p m j -> p (m j)"))
        odd_bf = keep.tile([P, 2 * P * PACK], BF16, name="odd_bf", tag=f"w1_bf{first_plane}", align_bytes=64)
        nc.vector.tensor_copy(
            odd_bf[:].rearrange("p (e m j) -> p m j e", e=2, j=PACK),
            w1_raw[:].rearrange("p (j m e o) -> p o m j e", j=PACK, e=2, o=2)[:, 1],
        )

        y = [keep.tile([P, S], F32, name=f"y{t}", align_bytes=64) for t in range(PACK)]

        def make_y(bank, t, lo, hi):
            acc = psum.tile([P, hi - lo], F32, name=f"acc_y{bank}", tag=f"bank{bank % BANKS}")
            product(acc[:], w1_code[t], w1_scale[t], x_code[:, lo:hi], x_scale[:, lo:hi])
            nc.scalar.copy(y[t][:, lo:hi], acc[:])

        pair = {t: keep.tile([P, 2 * V], F32, name=f"pair{t}", align_bytes=64) for t in PLANE_ORDER[1:]}
        terms = {}

        def new_terms(t):
            terms[t] = keep.tile([P, 2 * V], F32, name=f"terms{t}", tag="terms", align_bytes=64)

        def fetch(t, side):
            places = (la_sb, lb_sb)[side]
            nc.scalar.activation(pair[t][:, side * V : (side + 1) * V], y[t][:].indirect(places[:]), COPY)

        def make_and_fetch(bank, t):
            make_y(bank, t, 0, HALF)
            make_y(bank + 1, t, HALF, S)
            fetch(t, 0)
            fetch(t, 1)

        nc.scalar.activation(share[:, V:], share[:, 0:V], COPY, scale=-1.0, bias=1.0)
        for q in range(4):
            make_y(q, first_plane, q * QUARTER, (q + 1) * QUARTER)
        make_y(4, second_plane, 0, HALF)
        make_y(5, second_plane, HALF, S)
        fetch(second_plane, 1)
        nc.vector.quantize_mx(out=w1_codes[:, 2 * P :].bitcast(FP8X4), scales=w1_scales[:, 2 * P :], in_=odd_bf[:])
        make_and_fetch(6, third_plane)
        make_and_fetch(8, last_plane)

        w2_bf = [keep.tile([P, 2 * P, PACK], BF16, name=f"w2_bf{u}", align_bytes=64) for u in range(2)]
        w2_code = {}
        w2_scale = {}

        def cast_w2(m):
            nc.scalar.copy(
                w2_bf[m // 2][:, m % 2 * P : (m % 2 + 1) * P, :].rearrange("p (c i) j -> p c j i", i=4),
                w2_raw[:, :, m * P : (m + 1) * P].rearrange("p j (c i) -> p c j i", i=4),
            )

        def quantise_w2(u, code_tag, scale_tag):
            code = keep.tile([P, 2 * P], U32, name=f"w2_code{u}", tag=code_tag, align_bytes=64)
            scale = keep.tile([P, 2 * P], U8, name=f"w2_scale{u}", tag=scale_tag, align_bytes=64)
            nc.vector.quantize_mx(out=code[:].bitcast(FP8X4), scales=scale[:], in_=w2_bf[u][:].rearrange("p c j -> p (c j)"))
            for e in range(2):
                w2_code[2 * u + e] = code[:, e * P : (e + 1) * P]
                w2_scale[2 * u + e] = scale[:, e * P : (e + 1) * P]

        cast_w2(0)
        cast_w2(1)

        zs = {}
        mixes = keep.tile([P, 2 * V], F32, name="mixes", align_bytes=64)
        first_mix = keep.tile([P, V], F32, name="first_mix", align_bytes=64)
        mix = {first_plane: first_mix[:], second_plane: mixes[:, 0:V], third_plane: mixes[:, V:]}

        def weigh(t, lo, hi):
            nc.gpsimd.tensor_tensor(terms[t][:, lo:hi], pair[t][:, lo:hi], share[:, lo:hi], MULT)

        def add_terms(engine, t):
            engine.tensor_tensor(mix[t], terms[t][:, 0:V], terms[t][:, V:], ADD)

        def scatter_plane(t):
            zs[t] = keep.tile([P, S], F32, name=f"zs{t}", align_bytes=64)
            for places in (la_sb, lb_sb):
                nc.vector.tensor_copy(zs[t][:].indirect(places[:]), mix[t])

        def round_columns(t, h, lo, hi):
            nc.scalar.copy(zs_bf[h][:, lo:hi, t], zs[t][:, h * HALF + lo : h * HALF + hi])

        def round_plane(t):
            for h in range(2):
                round_columns(t, h, 0, HALF)

        new_terms(first_plane)
        for side, places in enumerate((la_sb, lb_sb)):
            cols = slice(side * V, (side + 1) * V)
            nc.vector.tensor_tensor(terms[first_plane][:, cols], y[first_plane][:].indirect(places[:]), share[:, cols], MULT)
        add_terms(nc.vector, first_plane)
        early_term = keep.tile([P, V], F32, name="early_term", align_bytes=64)
        for lo in (0, V // 2):
            cols = slice(lo, lo + V // 2)
            nc.vector.tensor_tensor(early_term[:, cols], y[second_plane][:].indirect(la_sb[:, lo // 16 : (lo + V // 2) // 16]), share[:, cols], MULT)
        terms[second_plane] = keep.tile([P, 2 * V], F32, name="second_terms", tag=f"y{second_plane}", align_bytes=64)
        weigh(second_plane, V, 2 * V)
        third_terms = [keep.tile([P, V], F32, name=f"third_term{side}", align_bytes=64) for side in range(2)]
        nc.gpsimd.tensor_tensor(third_terms[0][:], pair[third_plane][:, 0:V], share[:, 0:V], MULT)
        nc.gpsimd.tensor_tensor(mix[second_plane], early_term[:], terms[second_plane][:, V:], ADD)
        nc.gpsimd.tensor_tensor(third_terms[1][:], pair[third_plane][:, V:], share[:, V:], MULT)
        nc.gpsimd.tensor_tensor(mix[third_plane], third_terms[0][:], third_terms[1][:], ADD)
        for window, places in zip(windows, (la_sb, lb_sb)):
            nc.vector.tensor_copy(window[:].indirect(places[:]), mix[first_plane])
        zs[first_plane] = keep.tile([P, S], F32, name="first_sum", tag="third_term0", align_bytes=64)
        nc.gpsimd.tensor_tensor(zs[first_plane][:], windows[0][:], windows[1][:], ADD)
        terms[last_plane] = keep.tile([P, 2 * V], F32, name="last_terms", tag="third_term1", align_bytes=64)
        weigh(last_plane, 0, 2 * V)
        zs_bf = [keep.tile([P, HALF, PACK], BF16, name=f"zs_bf{h}", tag=f"window{h}", align_bytes=64) for h in range(2)]
        twins = (second_plane, third_plane)
        twin_mix = keep.tile([P, 2 * V], F32, name="twin_mix", align_bytes=64)
        nc.scalar.copy(twin_mix[:], mixes[:])
        round_plane(first_plane)
        cast_w2(2)
        cast_w2(3)
        for t in twins:
            zs[t] = keep.tile([P, S], F32, name=f"zs{t}", align_bytes=64)
            nc.vector.tensor_copy(zs[t][:].indirect(la_sb[:]), mix[t])
        last_mix = keep.tile([P, V], F32, name="last_mix", tag="mixes", align_bytes=64)
        mix[last_plane] = last_mix[:]
        add_terms(nc.gpsimd, last_plane)
        for n, t in enumerate(twins):
            nc.vector.tensor_copy(zs[t][:].indirect(lb_sb[:]), twin_mix[:, n * V : (n + 1) * V])
        for t in twins:
            round_plane(t)
        scatter_plane(last_plane)

        z_code = [keep.tile([P, HALF], U32, name=f"z_code{h}", align_bytes=64) for h in range(2)]
        z_scale = [keep.tile([P, HALF], U8, name=f"z_scale{h}", align_bytes=64) for h in range(2)]
        quarters = [(0, QUARTER), (QUARTER, HALF)]

        quantise_w2(0, "third_term1", "third_term0")
        for u in range(WARM_UPS):
            idle = psum.tile([WARM_UP_WIDTH, S], F32, name=f"idle{u}", tag=f"bank{BANKS - 1 - u}")
            product(idle[:], w2_code[0][:, 0:WARM_UP_WIDTH], w2_scale[0][:, 0:WARM_UP_WIDTH], w1_codes[:], w1_scales[:])
        quantise_w2(1, "w2_bf0", "w2_scale1")

        for lo, hi in quarters:
            nc.vector.tensor_copy(zs_bf[0][:, lo:hi, last_plane], zs[last_plane][:, lo:hi])
        nc.vector.tensor_copy(zs_bf[1][:, 0:LAST_ROUND_ON_VECTOR, last_plane], zs[last_plane][:, HALF : HALF + LAST_ROUND_ON_VECTOR])
        round_columns(last_plane, 1, LAST_ROUND_ON_VECTOR, HALF)
        for h in range(2):
            for lo, hi in quarters:
                nc.vector.quantize_mx(
                    out=z_code[h][:, lo:hi].bitcast(FP8X4), scales=z_scale[h][:, lo:hi], in_=zs_bf[h][:, lo:hi, :].rearrange("p c j -> p (c j)")
                )

        res = [keep.tile([P, S], F32, name=f"res{m}") for m in range(ROW_TILES)]
        last_tile = ROW_TILES - 1
        out_pieces = [(0, 0, lo, hi) for lo, hi in quarters] + [(m, 0, 0, HALF) for m in range(1, last_tile)]
        out_pieces = out_pieces + [(m, 1, 0, HALF) for m in range(last_tile)] + [(last_tile, h, 0, HALF) for h in range(2)]
        for n, (m, h, lo, hi) in enumerate(out_pieces):
            acc = psum.tile([P, hi - lo], F32, name=f"acc_out{n}", tag=f"bank{n % BANKS}")
            for c0, c1 in quarters if m < last_tile and hi - lo == HALF else [(lo, hi)]:
                product(acc[:, c0 - lo : c1 - lo], w2_code[m], w2_scale[m], z_code[h][:, c0:c1], z_scale[h][:, c0:c1])
            piece = res[m][:, h * HALF + lo : h * HALF + hi]
            if n >= OUT_PIECES_SCALAR_ALONE and (n - OUT_PIECES_SCALAR_ALONE) % 2 == 0:
                nc.vector.tensor_copy(piece, acc[:])
            else:
                nc.scalar.copy(piece, acc[:])
            if hi == HALF:
                cols = slice(h * HALF, (h + 1) * HALF)
                nc.sync.dma_start(out[m * P : (m + 1) * P, cols], res[m][:, cols])
